import numpy as np
import ml_dtypes


def mxq(x, axis, fmt="e4m3"):
    dtype, down = {"e4m3": (ml_dtypes.float8_e4m3fn, 7), "e5m2": (ml_dtypes.float8_e5m2, 14)}[fmt]
    v = np.moveaxis(np.asarray(x, np.float32).astype(ml_dtypes.bfloat16).astype(np.float64), axis, -1)
    blocks = v.reshape(v.shape[:-1] + (-1, 32))
    amax = np.abs(blocks).max(-1, keepdims=True)
    byte = np.maximum(np.where(amax > 0, np.frexp(amax)[1] - 1 + 127, 0) - down, 1)
    scale = np.exp2(byte - 127.0)
    codes = (blocks / scale).astype(np.float32).astype(dtype).astype(np.float64)
    return np.moveaxis((codes * scale).reshape(v.shape), -1, axis)


WIDE = False


def mx_kscale(k):
    if not WIDE:
        return np.ones(k)
    levels = np.array([24, -24, 12, -12, 0])
    if k % 512:
        return np.exp2(np.random.permutation(np.resize(levels, k // 32))).repeat(32)
    a = np.empty((k // 512, 16))
    for p in range(k // 512):
        a[p, :8] = np.random.permutation(np.resize(levels, 8))
        for g in range(8):
            far = levels[np.abs(levels - a[p, g]) >= 10]
            a[p, g + 8] = far[np.random.randint(len(far))]
    return np.exp2(a.ravel()).repeat(32)


def f64(x):
    return np.asarray(x).astype(np.float64)


def striped(idx):
    return np.tile(idx.reshape(-1, 16).T, (8, 1)).astype(np.uint16)


def unstriped(offs):
    return offs[:16].T.reshape(-1).astype(np.int64)


E2M1 = np.array([0.0, 0.5, 1.0, 1.5, 2.0, 3.0, 4.0, 6.0, -0.0, -0.5, -1.0, -1.5, -2.0, -3.0, -4.0, -6.0])


def pack_weight(w, fmt):
    k, n = w.shape
    w = f64(np.asarray(w, np.float32).astype(ml_dtypes.bfloat16)).reshape(k // 32, 32, n)
    amax = np.abs(w).max(1)
    if fmt == "e4m3":
        byte = np.frexp(amax)[1] - 1 + 127 - 7
    else:
        mant, ex = np.frexp(amax / 6.0)
        byte = np.where(mant > 0.5, ex, ex - 1) + 127
    byte = np.clip(np.where(amax > 0, byte, 1), 1, 254)
    scaled = (w * np.exp2(127.0 - byte)[:, None, :]).reshape(k, n).astype(np.float32)
    by_word = np.ascontiguousarray(scaled.reshape(k // 512, 128, 4, n).transpose(0, 1, 3, 2))
    if fmt == "e4m3":
        words = by_word.astype(ml_dtypes.float8_e4m3fn).view(np.uint8)
    else:
        c = by_word.astype(ml_dtypes.float4_e2m1fn).view(np.uint8) & 0xF
        words = (c[..., 0::2] | (c[..., 1::2] << 4)).reshape(k // 512, 128, 2 * n)
    return np.ascontiguousarray(words), np.ascontiguousarray(byte.astype(np.uint8).reshape(k // 512, 16, n))


def unpack_weight(words, scales, fmt):
    g, _, n = scales.shape
    words = np.ascontiguousarray(words).reshape(g, 128, n, -1)
    if fmt == "e4m3":
        vals = words.view(ml_dtypes.float8_e4m3fn).astype(np.float64)
    else:
        nib = np.empty((g, 128, n, 4), np.uint8)
        nib[..., 0::2] = words & 0xF
        nib[..., 1::2] = words >> 4
        vals = E2M1[nib]
    vals = vals * np.repeat(np.exp2(scales.astype(np.float64) - 127.0), 8, axis=1)[..., None]
    return vals.transpose(0, 1, 3, 2).reshape(g * 512, n)


def sigm(f):
    return 1.0 / (1.0 + np.exp(-np.maximum(f, -700.0)))


K, L, N, T, J = 512, 512, 512, 2048, 1024


def setup_inputs():
    n = np.random.standard_normal
    s = mx_kscale(K)[:, None]
    s2 = mx_kscale(L)[:, None]
    p_tab = pack_weight(n((K, T)) * s, "e4m3")
    p_tab2 = pack_weight(n((L, T)) * s2, "e4m3")
    return {
        "tab_words": p_tab[0],
        "tab_scales": p_tab[1],
        "tab2_words": p_tab2[0],
        "tab2_scales": p_tab2[1],
        "zv": (n((K, N)) / np.sqrt(K) / s).astype(np.float32),
        "zt": (n((L, N)) / np.sqrt(L) / s2).astype(np.float32),
        "b": (0.3 * n(N)).astype(np.float32),
        "wv": (n((K, N)) / np.sqrt(K) / s).astype(np.float32),
        "wt": (n((L, N)) / np.sqrt(L) / s2).astype(np.float32),
        "wgo": np.tile(np.random.uniform(0.5, 2.0, J), (128, 1)).astype(np.float32),
        "offs": striped(np.random.permutation(T)[:J]),
        "offs2": striped(np.random.permutation(T)[:J]),
    }


def reference(tab_words, tab_scales, tab2_words, tab2_scales, zv, zt, b, wv, wt, wgo, offs, offs2):
    idx = unstriped(offs)
    idx2 = unstriped(offs2)
    tab_ = unpack_weight(tab_words, tab_scales, "e4m3")[:, idx]
    tab2_ = unpack_weight(tab2_words, tab2_scales, "e4m3")[:, idx2]
    zv_ = mxq(f64(zv), 0, "e4m3")
    zt_ = mxq(f64(zt), 0, "e4m3")
    z = zv_.T @ tab_ + zt_.T @ tab2_
    gate = sigm(z + f64(b)[:, None])
    wv_ = mxq(f64(wv), 0, "e4m3")
    wt_ = mxq(f64(wt), 0, "e4m3")
    hv = wv_.T @ tab_
    ht = wt_.T @ tab2_
    av = np.tanh(hv)
    at = np.tanh(ht)
    out = np.zeros((N, T))
    out[:, idx] = f64(wgo)[0] * (at + gate * (av - at))
    return out

@@ -1,0 +1,228 @@
+from contextlib import ExitStack
+
+import concourse.mybir as mybir
+from concourse.masks import make_identity
+
+K, N, T, J = 512, 512, 2048, 1024
+FLOPS = 4 * 2 * K * N * J
+
+F32 = mybir.dt.float32
+BF16 = mybir.dt.bfloat16
+I32 = mybir.dt.int32
+U32 = mybir.dt.uint32
+U16 = mybir.dt.uint16
+U8 = mybir.dt.uint8
+FP8X4 = mybir.dt.float8_e4m3fn_x4
+ALU = mybir.AluOpType
+ACT = mybir.ActivationFunctionType
+
+P = 128
+PACK = 4
+HALF = 512
+N_TILES = N // P
+HALVES = J // HALF
+J_TILES = HALF // P
+LIST_COLS = HALF // 16
+WT, WV, ZV, ZT = range(4)
+PAGES = 2
+PLAIN = (0, 1)
+LAG_FROM = 8
+BLOCKS = ((0, 1), (1, 2), (2, 4))
+QUANT_AFTER = (0, 1, 2)
+HOLD = ()
+W_COLS = 1024
+W_ROW = 8
+
+
+def tile_list_gmu_tanh_scat_kernel(
+    tc, tab_words, tab_scales, tab2_words, tab2_scales, zv, zt, b, wv, wt, wgo, offs, offs2, out
+):
+    nc = tc.nc
+    weights = (wt, wv, zv, zt)
+    with ExitStack() as ctx:
+        held = ctx.enter_context(tc.tile_pool(name="held", bufs=1))
+        work = ctx.enter_context(tc.tile_pool(name="work", bufs=3))
+        psum = ctx.enter_context(tc.psum_pool(name="psum", bufs=1))
+
+        lists = [held.tile([P, J // 16], U16, name=f"list{a}") for a in range(2)]
+        words = [held.tile([P, T], I32, name=f"words{a}") for a in range(2)]
+        planes = [held.tile([P, T], U8, name=f"plane{a}") for a in range(2)]
+        nc.vector.memset(planes[0][:].bitcast(I32), 0)
+        nc.gpsimd.memset(planes[1][:].bitcast(I32), 0)
+        small = held.tile([P, P], F32)
+        nc.gpsimd.memset(small[:], 0.0)
+        for a, (lst, tw, ts) in enumerate(((offs, tab_words, tab_scales), (offs2, tab2_words, tab2_scales))):
+            nc.sync.dma_start(lists[a][:], lst)
+            nc.sync.dma_start(words[a][:], tw[0].rearrange("p t i -> p (t i)").bitcast(I32))
+            rows = ts[0].rearrange("(q r) t -> r q t", r=4)
+            for r in range(4):
+                nc.sync.dma_start(planes[a][r:P:32, :].bitcast(I32), rows[r].bitcast(I32))
+
+        raw = {}
+
+        def load_weights(t0, t1):
+            for w in range(4):
+                block = held.tile([P, PACK, (t1 - t0) * P], F32, name=f"raw{w}_{t0}")
+                nc.sync.dma_start(block[:], weights[w].rearrange("(p i) n -> p i n", i=PACK)[:, :, t0 * P : t1 * P])
+                for t in range(t0, t1):
+                    raw[t, w] = block[:, :, (t - t0) * P : (t - t0 + 1) * P]
+
+        load_weights(*BLOCKS[0])
+        nc.sync.dma_start(small[0:N_TILES, :], b.rearrange("(t p) -> t p", p=P))
+        nc.sync.dma_start(small[W_ROW : W_ROW + J // P, :], wgo[0].rearrange("(t p) -> t p", p=P))
+        w_rows = held.tile([P, W_COLS], F32)
+        for k, block in enumerate(BLOCKS[1:]):
+            if k == 1:
+                nc.sync.dma_start(w_rows[:], wgo[:, 0:W_COLS])
+            load_weights(*block)
+
+        ident = held.tile([P, P], F32)
+        make_identity(nc, ident[:])
+        pages = [held.tile([P, T], F32, name=f"page{g}") for g in range(PAGES)]
+        for page in pages:
+            nc.vector.memset(page[:].bitcast(I32), 0)
+
+        halves = held.tile([P, W_ROW + J // P], F32)
+        half_bias = halves[:, 0:N_TILES]
+        half_w = halves[:, W_ROW : W_ROW + J // P]
+
+        picked = {}
+        picked_scales = {}
+
+        def gather_words(a, h, tag):
+            t = held.tile([P, HALF], U32, name=f"picked{a}{h}", tag=tag, align_bytes=64)
+            entries = lists[a][:, h * LIST_COLS : (h + 1) * LIST_COLS]
+            nc.vector.tensor_copy(t[:], words[a][:].bitcast(U32).indirect(entries))
+            picked[a, h] = t
+
+        def gather_scales(a, h, t):
+            entries = lists[a][:, h * LIST_COLS : (h + 1) * LIST_COLS]
+            nc.vector.tensor_copy(t, planes[a][:].indirect(entries))
+            picked_scales[a, h] = t
+
+        codes = [held.tile([P, 4, P], U32, name=f"codes{t}", align_bytes=64) for t in range(N_TILES)]
+        scales = [held.tile([P, 4, P], U8, name=f"wscales{t}", align_bytes=64) for t in range(N_TILES)]
+
+        def quantise_weights(t):
+            for w0, group in (((0, 1), (1, 1), (2, 2)) if t == 0 else ((0, 2), (2, 2))):
+                tag = f"stage{w0}" if t == 0 else f"later{t}{w0}"
+                stage = held.tile([P, group, P * PACK], BF16, name=f"stage{t}{w0}", tag=tag, align_bytes=64)
+                for s in range(group):
+                    w = w0 + s
+                    nc.scalar.copy(
+                        stage[:, s, :].rearrange("p (c x i) -> p c i x", x=4, i=PACK),
+                        raw[t, w].rearrange("p i (c x) -> p c i x", x=4),
+                    )
+                nc.vector.quantize_mx(
+                    out=codes[t][:, w0 : w0 + group, :].rearrange("p w n -> p (w n)").bitcast(FP8X4),
+                    scales=scales[t][:, w0 : w0 + group, :].rearrange("p w n -> p (w n)"),
+                    in_=stage[:].rearrange("p w n -> p (w n)"),
+                )
+
+        def product_by_items(t, h, a, w, name):
+            acc = psum.tile([P, J_TILES, P], F32, name=name, tag=f"{name}{(t * HALVES + h) % 2}")
+            for q in range(J_TILES):
+                nc.tensor.matmul_mx(
+                    out=acc[:, q, :],
+                    lhsT=picked[a, h][:, q * P : (q + 1) * P].bitcast(FP8X4),
+                    lhsT_scale=picked_scales[a, h][:, q * P : (q + 1) * P],
+                    rhs=codes[t][:, w, :].bitcast(FP8X4),
+                    rhs_scale=scales[t][:, w, :],
+                    start=True,
+                    stop=True,
+                )
+            return acc
+
+        def unit(t, h):
+            step = t * HALVES + h
+            plain = step in PLAIN
+            ht = product_by_items(t, h, 1, WT, "ht")
+            hv = product_by_items(t, h, 0, WV, "hv")
+            z = psum.tile([P, HALF], F32, name="z", tag=f"z{step % 2}")
+            for a, w in ((0, ZV), (1, ZT)):
+                nc.tensor.matmul_mx(
+                    out=z[:],
+                    lhsT=codes[t][:, w, :].bitcast(FP8X4),
+                    lhsT_scale=scales[t][:, w, :],
+                    rhs=picked[a, h][:].bitcast(FP8X4),
+                    rhs_scale=picked_scales[a, h],
+                    start=(a == 0),
+                    stop=(a == 1),
+                )
+            acts = work.tile([P, 2, J_TILES, P], F32, name="acts")
+            nc.scalar.activation(acts[:, 0], ht[:], ACT.Tanh, scale=-1.0)
+            nc.scalar.activation(acts[:, 1], hv[:], ACT.Tanh)
+            if not plain:
+                scaled = work.tile([P, 2, J_TILES, P], F32, name="scaled")
+                for q in range(J_TILES):
+                    col = h * J_TILES + q
+                    nc.scalar.activation(
+                        scaled[:, :, q, :], acts[:, :, q, :], ACT.Copy, scale=half_w[:, col : col + 1]
+                    )
+                acts = scaled
+            u = work.tile([P, HALF], F32, name="u")
+            nc.scalar.activation(u[:], z[:], ACT.Tanh, bias=half_bias[:, t : t + 1], scale=0.5)
+            diff = psum.tile([P, J_TILES, P], F32, name="diff", tag=f"diff{step % 2}")
+            for q in range(J_TILES):
+                for s in range(2):
+                    nc.tensor.matmul(
+                        diff[:, q, :], acts[:, s, q, :], ident[:], start=(s == 0), stop=(s == 1), is_transpose=True
+                    )
+            gated = work.tile([P, HALF], F32, name="gated")
+            nc.vector.scalar_tensor_tensor(
+                gated[:], u[:], 1.0, diff[:].rearrange("p q j -> p (q j)"), ALU.add, ALU.mult
+            )
+            return gated, acts
+
+        def finish(t, h, gated, acts):
+            step = t * HALVES + h
+            plain = step in PLAIN
+            late = LAG_FROM <= step < N_TILES * HALVES - 1
+            tag = "ht1" if step == 0 else f"z{(step + late) % 2}"
+            neg = psum.tile([P, J_TILES, P], F32, name="neg", tag=tag)
+            for q in range(J_TILES):
+                nc.tensor.transpose(neg[:, q, :], acts[:, 0, q, :], ident[:])
+            page = pages[t % PAGES]
+            places = page[:].indirect(lists[0][:, h * LIST_COLS : (h + 1) * LIST_COLS])
+            if step in HOLD:
+                other = held.tile([P, HALF], F32, name="other", tag=f"later{1 + HOLD.index(step)}2", align_bytes=64)
+            else:
+                other = work.tile([P, HALF], F32, name="other")
+            if plain:
+                nc.vector.scalar_tensor_tensor(
+                    other[:], gated[:], 0.5, neg[:].rearrange("p q j -> p (q j)"), ALU.mult, ALU.subtract
+                )
+                nc.vector.tensor_tensor(places, other[:], w_rows[:, h * HALF : (h + 1) * HALF], ALU.mult)
+            else:
+                nc.scalar.activation(other[:], neg[:].rearrange("p q j -> p (q j)"), ACT.Copy, scale=-2.0)
+                nc.vector.tensor_tensor(places, gated[:], other[:], ALU.add)
+            if h == HALVES - 1:
+                nc.sync.dma_start(out[t * P : (t + 1) * P, :], page[:])
+
+        early_scales = held.tile([P, 2, HALF], U8, align_bytes=64)
+        for a in range(2):
+            gather_words(a, 0, f"early_words{a}")
+            gather_scales(a, 0, early_scales[:, a, :])
+        gather_words(0, 1, "late_words")
+        quantise_weights(0)
+        turned = psum.tile([P, P], F32, tag="diff1")
+        nc.tensor.transpose(turned[:], small[:], ident[:])
+        nc.scalar.mul(halves[:], turned[:, 0 : W_ROW + J // P], 0.5)
+        gather_words(1, 1, f"stage{WV}")
+        late_scales = held.tile([P, 2, HALF], U8, tag=f"stage{ZV}", align_bytes=64)
+        for a in (1, 0):
+            gather_scales(a, 1, late_scales[:, a, :])
+        waiting = None
+        for t in range(N_TILES):
+            for h in range(HALVES):
+                step = t * HALVES + h
+                made = unit(t, h)
+                if step in QUANT_AFTER:
+                    quantise_weights(1 + QUANT_AFTER.index(step))
+                if waiting is not None:
+                    finish(*waiting)
+                    waiting = None
+                if LAG_FROM <= step < N_TILES * HALVES - 1:
+                    waiting = (t, h) + made
+                else:
+                    finish(t, h, *made)

@@ -21,208 +21,335 @@ PACK = 4
 HALF = 512
 N_TILES = N // P
 HALVES = J // HALF
-J_TILES = HALF // P
 LIST_COLS = HALF // 16
-WT, WV, ZV, ZT = range(4)
+WV, WT, ZV, ZT = range(4)
 PAGES = 2
-PLAIN = (0, 1)
-LAG_FROM = 8
 BLOCKS = ((0, 1), (1, 2), (2, 4))
-QUANT_AFTER = (0, 1, 2)
-HOLD = ()
-W_COLS = 1024
 W_ROW = 8
+PLANE_ROW = (0, 4)
+ROUNDERS = ("ssss", "ssgg", "ggss", "gsss")
+STEPS = tuple((t, first, HALF) for t in range(N_TILES) for first in range(0, J, HALF))
+LOADS = "s0 t0 b0 s1 t1 w0 w1 w2 r0"
+KINDS = "vvooooot"
+SHORT = (0, 1)
+QUANT_AFTER = {0: 1, 2: 2, 4: 3}
+HOLD = {(0, "az"): "codes3", (1, "result"): "raw3_2", (3, "diff"): "stage2"}
+STAGE_TAG = {3: "stage2", 4: "stage2"}
+GROUPS = (((0, 0),), ((0, 1),), ((0, 2), (0, 3)), tuple((1, w) for w in range(4)), tuple((t, w) for t in (2, 3) for w in range(4)))
 
 
 def tile_list_gmu_tanh_scat_kernel(
     tc, tab_words, tab_scales, tab2_words, tab2_scales, zv, zt, b, wv, wt, wgo, offs, offs2, out
 ):
     nc = tc.nc
-    weights = (wt, wv, zv, zt)
+    weights = (wv, wt, zv, zt)
     with ExitStack() as ctx:
         held = ctx.enter_context(tc.tile_pool(name="held", bufs=1))
         work = ctx.enter_context(tc.tile_pool(name="work", bufs=3))
         psum = ctx.enter_context(tc.psum_pool(name="psum", bufs=1))
 
+        warm = held.tile([P, 2], F32)
+        nc.vector.memset(warm[:, 0:1], 0.0)
+        nc.scalar.activation(warm[:, 1:2], warm[:, 0:1], ACT.Sigmoid)
         lists = [held.tile([P, J // 16], U16, name=f"list{a}") for a in range(2)]
         words = [held.tile([P, T], I32, name=f"words{a}") for a in range(2)]
         planes = [held.tile([P, T], U8, name=f"plane{a}") for a in range(2)]
-        nc.vector.memset(planes[0][:].bitcast(I32), 0)
-        nc.gpsimd.memset(planes[1][:].bitcast(I32), 0)
+        for plane in planes:
+            nc.gpsimd.memset(plane[:].bitcast(I32), 0)
         small = held.tile([P, P], F32)
         nc.gpsimd.memset(small[:], 0.0)
-        for a, (lst, tw, ts) in enumerate(((offs, tab_words, tab_scales), (offs2, tab2_words, tab2_scales))):
+        for a, lst in enumerate((offs, offs2)):
             nc.sync.dma_start(lists[a][:], lst)
-            nc.sync.dma_start(words[a][:], tw[0].rearrange("p t i -> p (t i)").bitcast(I32))
-            rows = ts[0].rearrange("(q r) t -> r q t", r=4)
-            for r in range(4):
-                nc.sync.dma_start(planes[a][r:P:32, :].bitcast(I32), rows[r].bitcast(I32))
-
         raw = {}
+        tables = ((tab_words, tab_scales), (tab2_words, tab2_scales))
 
-        def load_weights(t0, t1):
+        def load_scales(a):
+            rows = tables[a][1][0].rearrange("(q r) t -> r q t", r=4)
+            for r in range(4):
+                row = PLANE_ROW[a] + r
+                nc.sync.dma_start(planes[a][row:P:32, :].bitcast(I32), rows[r].bitcast(I32))
+
+        def load_words(a):
+            nc.sync.dma_start(words[a][:], tables[a][0][0].rearrange("p t i -> p (t i)").bitcast(I32))
+
+        def load_small(a):
+            nc.sync.dma_start(small[0:N_TILES, :], b.rearrange("(t p) -> t p", p=P))
+            nc.sync.dma_start(small[W_ROW : W_ROW + J // P, :], wgo[0].rearrange("(t p) -> t p", p=P))
+
+        def load_weights(k):
+            t0, t1 = BLOCKS[k]
             for w in range(4):
-                block = held.tile([P, PACK, (t1 - t0) * P], F32, name=f"raw{w}_{t0}")
+                block = held.tile([P, PACK, (t1 - t0) * P], F32, name=f"raw{w}_{t0}", align_bytes=64)
                 nc.sync.dma_start(block[:], weights[w].rearrange("(p i) n -> p i n", i=PACK)[:, :, t0 * P : t1 * P])
                 for t in range(t0, t1):
                     raw[t, w] = block[:, :, (t - t0) * P : (t - t0 + 1) * P]
 
-        load_weights(*BLOCKS[0])
-        nc.sync.dma_start(small[0:N_TILES, :], b.rearrange("(t p) -> t p", p=P))
-        nc.sync.dma_start(small[W_ROW : W_ROW + J // P, :], wgo[0].rearrange("(t p) -> t p", p=P))
-        w_rows = held.tile([P, W_COLS], F32)
-        for k, block in enumerate(BLOCKS[1:]):
-            if k == 1:
-                nc.sync.dma_start(w_rows[:], wgo[:, 0:W_COLS])
-            load_weights(*block)
+        w_rows = held.tile([P, J], F32)
+
+        def load_rows(a):
+            nc.sync.dma_start(w_rows[:], wgo)
+
+        loaders = {"r": load_rows, "s": load_scales, "t": load_words, "b": load_small, "w": load_weights}
+        for item in LOADS.split():
+            loaders[item[0]](int(item[1]))
 
         ident = held.tile([P, P], F32)
         make_identity(nc, ident[:])
         pages = [held.tile([P, T], F32, name=f"page{g}") for g in range(PAGES)]
         for page in pages:
-            nc.vector.memset(page[:].bitcast(I32), 0)
+            nc.gpsimd.memset(page[:].bitcast(I32), 0)
 
-        halves = held.tile([P, W_ROW + J // P], F32)
-        half_bias = halves[:, 0:N_TILES]
-        half_w = halves[:, W_ROW : W_ROW + J // P]
+        columns = held.tile([P, W_ROW + J // P], F32)
+        bias = columns[:, 0:N_TILES]
+        w_cols = columns[:, W_ROW:]
 
         picked = {}
         picked_scales = {}
 
         def gather_words(a, h, tag):
-            t = held.tile([P, HALF], U32, name=f"picked{a}{h}", tag=tag, align_bytes=64)
+            t = held.tile([P, HALF], U32, name=f"gw{a}{h}", tag=tag, align_bytes=64)
             entries = lists[a][:, h * LIST_COLS : (h + 1) * LIST_COLS]
             nc.vector.tensor_copy(t[:], words[a][:].bitcast(U32).indirect(entries))
             picked[a, h] = t
 
-        def gather_scales(a, h, t):
+        def gather_scales(a, h, tag):
+            t = held.tile([P, HALF], U8, name=f"gs{a}{h}", tag=tag, align_bytes=64)
             entries = lists[a][:, h * LIST_COLS : (h + 1) * LIST_COLS]
-            nc.vector.tensor_copy(t, planes[a][:].indirect(entries))
-            picked_scales[a, h] = t
+            nc.vector.tensor_copy(t[:], planes[a][:].indirect(entries))
+            picked_scales[a, h] = t[PLANE_ROW[a] : P, :]
 
-        codes = [held.tile([P, 4, P], U32, name=f"codes{t}", align_bytes=64) for t in range(N_TILES)]
-        scales = [held.tile([P, 4, P], U8, name=f"wscales{t}", align_bytes=64) for t in range(N_TILES)]
+        codes = {}
+        scales = {}
 
-        def quantise_weights(t):
-            for w0, group in (((0, 1), (1, 1), (2, 2)) if t == 0 else ((0, 2), (2, 2))):
-                tag = f"stage{w0}" if t == 0 else f"later{t}{w0}"
-                stage = held.tile([P, group, P * PACK], BF16, name=f"stage{t}{w0}", tag=tag, align_bytes=64)
-                for s in range(group):
-                    w = w0 + s
-                    nc.scalar.copy(
-                        stage[:, s, :].rearrange("p (c x i) -> p c i x", x=4, i=PACK),
-                        raw[t, w].rearrange("p i (c x) -> p c i x", x=4),
-                    )
-                nc.vector.quantize_mx(
-                    out=codes[t][:, w0 : w0 + group, :].rearrange("p w n -> p (w n)").bitcast(FP8X4),
-                    scales=scales[t][:, w0 : w0 + group, :].rearrange("p w n -> p (w n)"),
-                    in_=stage[:].rearrange("p w n -> p (w n)"),
+        def round_weight(dst, t, w):
+            engine = ROUNDERS[t][w]
+            if engine == "g":
+                nc.gpsimd.tensor_scalar(
+                    dst.rearrange("p (n i) -> p n i", i=PACK),
+                    raw[t, w].rearrange("p i n -> p n i"),
+                    1.0,
+                    0.0,
+                    ALU.mult,
+                    ALU.add,
+                )
+            else:
+                copy = nc.scalar.copy if engine == "s" else nc.vector.tensor_copy
+                copy(
+                    dst.rearrange("p (c x i) -> p c i x", x=4, i=PACK),
+                    raw[t, w].rearrange("p i (c x) -> p c i x", x=4),
                 )
 
-        def product_by_items(t, h, a, w, name):
-            acc = psum.tile([P, J_TILES, P], F32, name=name, tag=f"{name}{(t * HALVES + h) % 2}")
-            for q in range(J_TILES):
+        stages = {}
+
+        def round_piece(t, w):
+            for g, pieces in enumerate(GROUPS):
+                if (t, w) in pieces:
+                    if g not in stages:
+                        tag = STAGE_TAG.get(g, f"stage{g}")
+                        shape = [P, len(pieces), P * PACK]
+                        stages[g] = held.tile(shape, BF16, name=f"st{g}", tag=tag, align_bytes=64)
+                    round_weight(stages[g][:, pieces.index((t, w)), :], t, w)
+
+        def quantise(g):
+            pieces = GROUPS[g]
+            group_codes = held.tile([P, len(pieces), P], U32, name=f"codes{g}", align_bytes=64)
+            group_scales = held.tile([P, len(pieces), P], U8, name=f"wscales{g}", align_bytes=64)
+            nc.vector.quantize_mx(
+                out=group_codes[:].rearrange("p w n -> p (w n)").bitcast(FP8X4),
+                scales=group_scales[:].rearrange("p w n -> p (w n)"),
+                in_=stages[g][:].rearrange("p w n -> p (w n)"),
+            )
+            for n, piece in enumerate(pieces):
+                codes[piece] = group_codes[:, n, :]
+                scales[piece] = group_scales[:, n, :]
+
+        def quantise_weights(t):
+            for g, pieces in enumerate(GROUPS):
+                if pieces[0][0] == t:
+                    for piece in pieces:
+                        round_piece(*piece)
+                    quantise(g)
+
+        made = {}
+
+        def scratch(step, name):
+            if (step, name) in HOLD:
+                made[step, name] = held.tile([P, STEPS[step][2]], F32, name=f"{name}{step}", tag=HOLD[step, name], align_bytes=64)
+            else:
+                made[step, name] = work.tile([P, STEPS[step][2]], F32, name=f"{name}{step}", tag=name)
+            return made[step, name]
+
+        def activate(step, name, passes):
+            t, first, width = STEPS[step]
+            h, lo = divmod(first, HALF)
+            acc = psum.tile([P, width], F32, name=f"{name}{step}", tag=name)
+            for n, (a, w) in enumerate(passes):
+                nc.tensor.matmul_mx(
+                    out=acc[:],
+                    lhsT=codes[t, w].bitcast(FP8X4),
+                    lhsT_scale=scales[t, w],
+                    rhs=picked[a, h][:, lo : lo + width].bitcast(FP8X4),
+                    rhs_scale=picked_scales[a, h][:, lo : lo + width],
+                    start=(n == 0),
+                    stop=(n == len(passes) - 1),
+                )
+            act = scratch(step, f"a{name}")
+            if name == "z":
+                nc.scalar.activation(act[:], acc[:], ACT.Sigmoid, bias=bias[:, t : t + 1])
+            else:
+                nc.scalar.activation(act[:], acc[:], ACT.Tanh)
+
+        def mix(step):
+            diff = scratch(step, "diff")
+            nc.gpsimd.tensor_tensor(diff[:], made[step, "ahv"][:], made[step, "aht"][:], ALU.subtract)
+            gated = scratch(step, "gated")
+            nc.gpsimd.tensor_tensor(gated[:], diff[:], made[step, "az"][:], ALU.mult)
+
+        def activate_by_entries(step, name, a, w, sign):
+            t, first, width = STEPS[step]
+            h, lo = divmod(first, HALF)
+            acc = psum.tile([P, width // P, P], F32, name=f"{name}{step}", tag=name)
+            for q in range(width // P):
+                cols = slice(lo + q * P, lo + (q + 1) * P)
                 nc.tensor.matmul_mx(
                     out=acc[:, q, :],
-                    lhsT=picked[a, h][:, q * P : (q + 1) * P].bitcast(FP8X4),
-                    lhsT_scale=picked_scales[a, h][:, q * P : (q + 1) * P],
-                    rhs=codes[t][:, w, :].bitcast(FP8X4),
-                    rhs_scale=scales[t][:, w, :],
+                    lhsT=picked[a, h][:, cols].bitcast(FP8X4),
+                    lhsT_scale=picked_scales[a, h][:, cols],
+                    rhs=codes[t, w].bitcast(FP8X4),
+                    rhs_scale=scales[t, w],
                     start=True,
                     stop=True,
                 )
-            return acc
+            act = scratch(step, f"a{name}")
+            nc.scalar.activation(act[:], acc[:].rearrange("p q j -> p (q j)"), ACT.Tanh, scale=sign)
 
-        def unit(t, h):
-            step = t * HALVES + h
-            plain = step in PLAIN
-            ht = product_by_items(t, h, 1, WT, "ht")
-            hv = product_by_items(t, h, 0, WV, "hv")
-            z = psum.tile([P, HALF], F32, name="z", tag=f"z{step % 2}")
-            for a, w in ((0, ZV), (1, ZT)):
-                nc.tensor.matmul_mx(
-                    out=z[:],
-                    lhsT=codes[t][:, w, :].bitcast(FP8X4),
-                    lhsT_scale=scales[t][:, w, :],
-                    rhs=picked[a, h][:].bitcast(FP8X4),
-                    rhs_scale=picked_scales[a, h],
-                    start=(a == 0),
-                    stop=(a == 1),
-                )
-            acts = work.tile([P, 2, J_TILES, P], F32, name="acts")
-            nc.scalar.activation(acts[:, 0], ht[:], ACT.Tanh, scale=-1.0)
-            nc.scalar.activation(acts[:, 1], hv[:], ACT.Tanh)
-            if not plain:
-                scaled = work.tile([P, 2, J_TILES, P], F32, name="scaled")
-                for q in range(J_TILES):
-                    col = h * J_TILES + q
-                    nc.scalar.activation(
-                        scaled[:, :, q, :], acts[:, :, q, :], ACT.Copy, scale=half_w[:, col : col + 1]
-                    )
-                acts = scaled
-            u = work.tile([P, HALF], F32, name="u")
-            nc.scalar.activation(u[:], z[:], ACT.Tanh, bias=half_bias[:, t : t + 1], scale=0.5)
-            diff = psum.tile([P, J_TILES, P], F32, name="diff", tag=f"diff{step % 2}")
-            for q in range(J_TILES):
-                for s in range(2):
+        def turn(step, tag, names):
+            tiles = STEPS[step][2] // P
+            bank = psum.tile([P, tiles, P], F32, name=f"{tag}{step}", tag=f"{tag}{step % 2}")
+            for q in range(tiles):
+                for s, name in enumerate(names):
                     nc.tensor.matmul(
-                        diff[:, q, :], acts[:, s, q, :], ident[:], start=(s == 0), stop=(s == 1), is_transpose=True
+                        bank[:, q, :],
+                        made[step, name][:, q * P : (q + 1) * P],
+                        ident[:],
+                        start=(s == 0),
+                        stop=(s == len(names) - 1),
+                        is_transpose=True,
                     )
-            gated = work.tile([P, HALF], F32, name="gated")
-            nc.vector.scalar_tensor_tensor(
-                gated[:], u[:], 1.0, diff[:].rearrange("p q j -> p (q j)"), ALU.add, ALU.mult
-            )
-            return gated, acts
+            return bank[:].rearrange("p q j -> p (q j)")
 
-        def finish(t, h, gated, acts):
-            step = t * HALVES + h
-            plain = step in PLAIN
-            late = LAG_FROM <= step < N_TILES * HALVES - 1
-            tag = "ht1" if step == 0 else f"z{(step + late) % 2}"
-            neg = psum.tile([P, J_TILES, P], F32, name="neg", tag=tag)
-            for q in range(J_TILES):
-                nc.tensor.transpose(neg[:, q, :], acts[:, 0, q, :], ident[:])
-            page = pages[t % PAGES]
-            places = page[:].indirect(lists[0][:, h * LIST_COLS : (h + 1) * LIST_COLS])
-            if step in HOLD:
-                other = held.tile([P, HALF], F32, name="other", tag=f"later{1 + HOLD.index(step)}2", align_bytes=64)
-            else:
-                other = work.tile([P, HALF], F32, name="other")
-            if plain:
-                nc.vector.scalar_tensor_tensor(
-                    other[:], gated[:], 0.5, neg[:].rearrange("p q j -> p (q j)"), ALU.mult, ALU.subtract
+        def spread_w(h, tag):
+            spread = psum.tile([P, HALF // P, P], F32, name=f"spread{h}", tag=tag)
+            for q in range(HALF // P):
+                col = h * HALF // P + q
+                nc.tensor.transpose(spread[:, q, :], w_cols[:, col : col + 1].to_broadcast([P, P]), ident[:])
+            return spread[:].rearrange("p q j -> p (q j)")
+
+        def mix_short(step):
+            t, first, width = STEPS[step]
+            both = turn(step, "total", ("aht", "ahv"))
+            rest = turn(step, "back", ("aht",))
+            gated = scratch(step, "gated")
+            nc.vector.tensor_tensor(gated[:], made[step, "az"][:], both, ALU.mult)
+            mixed = scratch(step, "diff")
+            nc.vector.tensor_tensor(mixed[:], gated[:], rest, ALU.subtract)
+
+        def weigh_short(step):
+            first = STEPS[step][1]
+            result = scratch(step, "result")
+            nc.vector.tensor_tensor(result[:], made[step, "diff"][:], spread_w(first // HALF, "turned"), ALU.mult)
+
+        def add_last(step):
+            result = scratch(step, "result")
+            nc.gpsimd.tensor_tensor(result[:], made[step, "gated"][:], made[step, "aht"][:], ALU.add)
+
+        def weigh(step):
+            t, first, width = STEPS[step]
+            tiles = width // P
+            total = psum.tile([P, tiles, P], F32, name=f"total{step}", tag=f"total{step % 2}")
+            for q in range(tiles):
+                for s, name in enumerate(("gated", "aht")):
+                    nc.tensor.matmul(
+                        total[:, q, :],
+                        made[step, name][:, q * P : (q + 1) * P],
+                        ident[:],
+                        start=(s == 0),
+                        stop=(s == 1),
+                        is_transpose=True,
+                    )
+            weighed = scratch(step, "weighed")
+            for q in range(tiles):
+                col = first // P + q
+                nc.scalar.activation(
+                    weighed[:, q * P : (q + 1) * P],
+                    total[:, q, :],
+                    ACT.Copy,
+                    scale=w_cols[:, col : col + 1],
                 )
-                nc.vector.tensor_tensor(places, other[:], w_rows[:, h * HALF : (h + 1) * HALF], ALU.mult)
+
+        def turn_back(step):
+            tiles = STEPS[step][2] // P
+            weighed = made[step, "weighed"]
+            back = psum.tile([P, tiles, P], F32, name=f"back{step}", tag=f"back{step % 2}")
+            for q in range(tiles):
+                nc.tensor.transpose(back[:, q, :], weighed[:, q * P : (q + 1) * P], ident[:])
+            result = scratch(step, "result")
+            nc.scalar.copy(result[:], back[:].rearrange("p q j -> p (q j)"))
+
+        def place(step):
+            t, first, width = STEPS[step]
+            page = pages[t % PAGES]
+            places = page[:].indirect(lists[0][:, first // 16 : (first + width) // 16])
+            if KINDS[step] == "t":
+                nc.vector.tensor_tensor(places, made[step, "result"][:], w_rows[:, first : first + width], ALU.mult)
             else:
-                nc.scalar.activation(other[:], neg[:].rearrange("p q j -> p (q j)"), ACT.Copy, scale=-2.0)
-                nc.vector.tensor_tensor(places, gated[:], other[:], ALU.add)
-            if h == HALVES - 1:
+                nc.vector.tensor_copy(places, made[step, "result"][:])
+            if first + width == J:
                 nc.sync.dma_start(out[t * P : (t + 1) * P, :], page[:])
 
-        early_scales = held.tile([P, 2, HALF], U8, align_bytes=64)
-        for a in range(2):
-            gather_words(a, 0, f"early_words{a}")
-            gather_scales(a, 0, early_scales[:, a, :])
-        gather_words(0, 1, "late_words")
-        quantise_weights(0)
-        turned = psum.tile([P, P], F32, tag="diff1")
+        gather_scales(0, 0, "gs00")
+        gather_scales(0, 1, "gs01")
+        gather_words(0, 0, "gw00")
+        gather_scales(1, 0, "gs10")
+        gather_words(1, 0, "gw10")
+        gather_words(0, 1, "gw01")
+        turned = psum.tile([P, P], F32, tag="turned")
         nc.tensor.transpose(turned[:], small[:], ident[:])
-        nc.scalar.mul(halves[:], turned[:, 0 : W_ROW + J // P], 0.5)
-        gather_words(1, 1, f"stage{WV}")
-        late_scales = held.tile([P, 2, HALF], U8, tag=f"stage{ZV}", align_bytes=64)
-        for a in (1, 0):
-            gather_scales(a, 1, late_scales[:, a, :])
-        waiting = None
-        for t in range(N_TILES):
-            for h in range(HALVES):
-                step = t * HALVES + h
-                made = unit(t, h)
-                if step in QUANT_AFTER:
-                    quantise_weights(1 + QUANT_AFTER.index(step))
-                if waiting is not None:
-                    finish(*waiting)
-                    waiting = None
-                if LAG_FROM <= step < N_TILES * HALVES - 1:
-                    waiting = (t, h) + made
+        nc.scalar.copy(columns[:], turned[:, 0 : W_ROW + J // P])
+        quantise_weights(0)
+        gather_scales(1, 1, "stage1")
+        gather_words(1, 1, f"raw{ZT}_0")
+        for tok in """v0 t0 z0 M0 r10 r11 r12 r13 q3 W0 v1 t1 z1 P0 r20 r30 r21 v2 t2 z2 M2 M1 r31 r22 r32 r23 r33 q4 W1 P1 v3 t3 z3 M3 W2 B2 P2 v4 t4 z4 M4 W3 B3 P3 v5 t5 z5 M5 W4 B4 P4 v6 t6 z6 M6 W5 B5 P5 v7 t7 z7 M7 W7 W6 B6 P6 P7""".split():
+            k, step = tok[0], int(tok[1])
+            if k == "v":
+                if KINDS[step] != "v":
+                    activate(step, "hv", ((0, WV),))
                 else:
-                    finish(t, h, *made)
+                    activate_by_entries(step, "hv", 0, WV, 1.0)
+            elif k == "t":
+                if KINDS[step] != "v":
+                    activate(step, "ht", ((1, WT),))
+                else:
+                    activate_by_entries(step, "ht", 1, WT, -1.0)
+            elif k == "z":
+                activate(step, "z", ((0, ZV), (1, ZT)))
+            elif k == "M":
+                if KINDS[step] != "v":
+                    mix(step)
+                else:
+                    mix_short(step)
+            elif k == "W":
+                if KINDS[step] == "o":
+                    weigh(step)
+                elif KINDS[step] == "t":
+                    add_last(step)
+                else:
+                    weigh_short(step)
+            elif k == "B":
+                turn_back(step)
+            elif k == "P":
+                place(step)
+            elif k == "r":
+                round_piece(step, int(tok[2]))
+            elif k == "q":
+                quantise(step)

@@ -27,15 +27,16 @@ PAGES = 2
 BLOCKS = ((0, 1), (1, 2), (2, 4))
 W_ROW = 8
 PLANE_ROW = (0, 4)
-ROUNDERS = ("ssss", "ssgg", "ggss", "gsss")
+ROUNDERS = ("ssss", "ssvv", "ggss", "ssss")
 STEPS = tuple((t, first, HALF) for t in range(N_TILES) for first in range(0, J, HALF))
 LOADS = "s0 t0 b0 s1 t1 w0 w1 w2 r0"
 KINDS = "vvooooot"
 SHORT = (0, 1)
 QUANT_AFTER = {0: 1, 2: 2, 4: 3}
-HOLD = {(0, "az"): "codes3", (1, "result"): "raw3_2", (3, "diff"): "stage2"}
-STAGE_TAG = {3: "stage2", 4: "stage2"}
-GROUPS = (((0, 0),), ((0, 1),), ((0, 2), (0, 3)), tuple((1, w) for w in range(4)), tuple((t, w) for t in (2, 3) for w in range(4)))
+HOLD = {(0, "az"): "codes4", (0, "aht"): "late", (1, "result"): "raw3_2", (3, "diff"): "late"}
+STAGE_TAG = {4: "stage2", 5: "late"}
+BANK = {}
+GROUPS = tuple(((0, w),) for w in range(4)) + (tuple((1, w) for w in range(4)), tuple((t, w) for t in (2, 3) for w in range(4)))
 
 
 def tile_list_gmu_tanh_scat_kernel(
@@ -208,7 +209,7 @@ def tile_list_gmu_tanh_scat_kernel(
         def activate_by_entries(step, name, a, w, sign):
             t, first, width = STEPS[step]
             h, lo = divmod(first, HALF)
-            acc = psum.tile([P, width // P, P], F32, name=f"{name}{step}", tag=name)
+            acc = psum.tile([P, width // P, P], F32, name=f"{name}{step}", tag=BANK.get((step, name), name))
             for q in range(width // P):
                 cols = slice(lo + q * P, lo + (q + 1) * P)
                 nc.tensor.matmul_mx(
@@ -248,9 +249,12 @@ def tile_list_gmu_tanh_scat_kernel(
         def mix_short(step):
             t, first, width = STEPS[step]
             both = turn(step, "total", ("aht", "ahv"))
-            rest = turn(step, "back", ("aht",))
             gated = scratch(step, "gated")
             nc.vector.tensor_tensor(gated[:], made[step, "az"][:], both, ALU.mult)
+
+        def add_short(step):
+            gated = made[step, "gated"]
+            rest = turn(step, "back", ("aht",))
             mixed = scratch(step, "diff")
             nc.vector.tensor_tensor(mixed[:], gated[:], rest, ALU.subtract)
 
@@ -319,7 +323,7 @@ def tile_list_gmu_tanh_scat_kernel(
         quantise_weights(0)
         gather_scales(1, 1, "stage1")
         gather_words(1, 1, f"raw{ZT}_0")
-        for tok in """v0 t0 z0 M0 r10 r11 r12 r13 q3 W0 v1 t1 z1 P0 r20 r30 r21 v2 t2 z2 M2 M1 r31 r22 r32 r23 r33 q4 W1 P1 v3 t3 z3 M3 W2 B2 P2 v4 t4 z4 M4 W3 B3 P3 v5 t5 z5 M5 W4 B4 P4 v6 t6 z6 M6 W5 B5 P5 v7 t7 z7 M7 W7 W6 B6 P6 P7""".split():
+        for tok in """v0 t0 z0 M0 r10 r11 r12 r13 v1 t1 N0 q4 W0 z1 P0 r20 r21 r30 v2 t2 z2 M2 M1 N1 r31 r22 r32 r23 r33 q5 W1 P1 v3 t3 z3 M3 W2 B2 P2 v4 t4 z4 M4 W3 B3 P3 v5 t5 z5 M5 W4 B4 P4 v6 t6 z6 M6 W5 B5 P5 v7 t7 z7 M7 W7 W6 B6 P6 P7""".split():
             k, step = tok[0], int(tok[1])
             if k == "v":
                 if KINDS[step] != "v":
@@ -345,6 +349,8 @@ def tile_list_gmu_tanh_scat_kernel(
                     add_last(step)
                 else:
                     weigh_short(step)
+            elif k == "N":
+                add_short(step)
             elif k == "B":
                 turn_back(step)
             elif k == "P":

@@ -20,23 +20,15 @@ P = 128
 PACK = 4
 HALF = 512
 N_TILES = N // P
-HALVES = J // HALF
+QUARTERS = HALF // P
 LIST_COLS = HALF // 16
 WV, WT, ZV, ZT = range(4)
-PAGES = 2
 BLOCKS = ((0, 1), (1, 2), (2, 4))
 W_ROW = 8
 PLANE_ROW = (0, 4)
+PAGES = 2
+STEPS = tuple((t, h) for t in range(N_TILES) for h in range(2))
 ROUNDERS = ("ssss", "ssvv", "ggss", "ssss")
-STEPS = tuple((t, first, HALF) for t in range(N_TILES) for first in range(0, J, HALF))
-LOADS = "s0 t0 b0 s1 t1 w0 w1 w2 r0"
-KINDS = "vvooooot"
-SHORT = (0, 1)
-QUANT_AFTER = {0: 1, 2: 2, 4: 3}
-HOLD = {(0, "az"): "codes4", (0, "aht"): "late", (1, "result"): "raw3_2", (3, "diff"): "late"}
-STAGE_TAG = {4: "stage2", 5: "late"}
-BANK = {}
-GROUPS = tuple(((0, w),) for w in range(4)) + (tuple((1, w) for w in range(4)), tuple((t, w) for t in (2, 3) for w in range(4)))
 
 
 def tile_list_gmu_tanh_scat_kernel(
@@ -52,6 +44,7 @@ def tile_list_gmu_tanh_scat_kernel(
         warm = held.tile([P, 2], F32)
         nc.vector.memset(warm[:, 0:1], 0.0)
         nc.scalar.activation(warm[:, 1:2], warm[:, 0:1], ACT.Sigmoid)
+
         lists = [held.tile([P, J // 16], U16, name=f"list{a}") for a in range(2)]
         words = [held.tile([P, T], I32, name=f"words{a}") for a in range(2)]
         planes = [held.tile([P, T], U8, name=f"plane{a}") for a in range(2)]
@@ -59,256 +52,189 @@ def tile_list_gmu_tanh_scat_kernel(
             nc.gpsimd.memset(plane[:].bitcast(I32), 0)
         small = held.tile([P, P], F32)
         nc.gpsimd.memset(small[:], 0.0)
-        for a, lst in enumerate((offs, offs2)):
-            nc.sync.dma_start(lists[a][:], lst)
-        raw = {}
-        tables = ((tab_words, tab_scales), (tab2_words, tab2_scales))
 
-        def load_scales(a):
-            rows = tables[a][1][0].rearrange("(q r) t -> r q t", r=4)
+        def load_table(a, table_words, table_scales):
+            rows = table_scales[0].rearrange("(q r) t -> r q t", r=4)
             for r in range(4):
-                row = PLANE_ROW[a] + r
-                nc.sync.dma_start(planes[a][row:P:32, :].bitcast(I32), rows[r].bitcast(I32))
+                nc.sync.dma_start(planes[a][PLANE_ROW[a] + r : P : 32, :].bitcast(I32), rows[r].bitcast(I32))
+            nc.sync.dma_start(words[a][:], table_words[0].rearrange("p t i -> p (t i)").bitcast(I32))
 
-        def load_words(a):
-            nc.sync.dma_start(words[a][:], tables[a][0][0].rearrange("p t i -> p (t i)").bitcast(I32))
-
-        def load_small(a):
-            nc.sync.dma_start(small[0:N_TILES, :], b.rearrange("(t p) -> t p", p=P))
-            nc.sync.dma_start(small[W_ROW : W_ROW + J // P, :], wgo[0].rearrange("(t p) -> t p", p=P))
-
-        def load_weights(k):
-            t0, t1 = BLOCKS[k]
+        nc.sync.dma_start(lists[0][:], offs)
+        nc.sync.dma_start(lists[1][:], offs2)
+        load_table(0, tab_words, tab_scales)
+        load_table(1, tab2_words, tab2_scales)
+        nc.sync.dma_start(small[0:N_TILES, :], b.rearrange("(t p) -> t p", p=P))
+        nc.sync.dma_start(small[W_ROW : W_ROW + J // P, :], wgo[0].rearrange("(t p) -> t p", p=P))
+        raw = {}
+        for t0, t1 in BLOCKS:
             for w in range(4):
                 block = held.tile([P, PACK, (t1 - t0) * P], F32, name=f"raw{w}_{t0}", align_bytes=64)
                 nc.sync.dma_start(block[:], weights[w].rearrange("(p i) n -> p i n", i=PACK)[:, :, t0 * P : t1 * P])
                 for t in range(t0, t1):
                     raw[t, w] = block[:, :, (t - t0) * P : (t - t0 + 1) * P]
-
-        w_rows = held.tile([P, J], F32)
-
-        def load_rows(a):
-            nc.sync.dma_start(w_rows[:], wgo)
-
-        loaders = {"r": load_rows, "s": load_scales, "t": load_words, "b": load_small, "w": load_weights}
-        for item in LOADS.split():
-            loaders[item[0]](int(item[1]))
+        w_rows = held.tile([P, HALF], F32)
+        nc.sync.dma_start(w_rows[:], wgo[:, STEPS[-1][1] * HALF : (STEPS[-1][1] + 1) * HALF])
 
         ident = held.tile([P, P], F32)
         make_identity(nc, ident[:])
         pages = [held.tile([P, T], F32, name=f"page{g}") for g in range(PAGES)]
         for page in pages:
-            nc.gpsimd.memset(page[:].bitcast(I32), 0)
-
-        columns = held.tile([P, W_ROW + J // P], F32)
-        bias = columns[:, 0:N_TILES]
-        w_cols = columns[:, W_ROW:]
+            nc.vector.memset(page[:].bitcast(I32), 0)
 
         picked = {}
         picked_scales = {}
 
         def gather_words(a, h, tag):
-            t = held.tile([P, HALF], U32, name=f"gw{a}{h}", tag=tag, align_bytes=64)
+            tile = held.tile([P, HALF], U32, name=f"gw{a}{h}", tag=tag, align_bytes=64)
             entries = lists[a][:, h * LIST_COLS : (h + 1) * LIST_COLS]
-            nc.vector.tensor_copy(t[:], words[a][:].bitcast(U32).indirect(entries))
-            picked[a, h] = t
+            nc.vector.tensor_copy(tile[:], words[a][:].bitcast(U32).indirect(entries))
+            picked[a, h] = tile
 
         def gather_scales(a, h, tag):
-            t = held.tile([P, HALF], U8, name=f"gs{a}{h}", tag=tag, align_bytes=64)
+            tile = held.tile([P, HALF], U8, name=f"gs{a}{h}", tag=tag, align_bytes=64)
             entries = lists[a][:, h * LIST_COLS : (h + 1) * LIST_COLS]
-            nc.vector.tensor_copy(t[:], planes[a][:].indirect(entries))
-            picked_scales[a, h] = t[PLANE_ROW[a] : P, :]
+            nc.vector.tensor_copy(tile[:], planes[a][:].indirect(entries))
+            picked_scales[a, h] = tile[PLANE_ROW[a] : P, :]
 
         codes = {}
         scales = {}
 
-        def round_weight(dst, t, w):
-            engine = ROUNDERS[t][w]
-            if engine == "g":
-                nc.gpsimd.tensor_scalar(
-                    dst.rearrange("p (n i) -> p n i", i=PACK),
-                    raw[t, w].rearrange("p i n -> p n i"),
-                    1.0,
-                    0.0,
-                    ALU.mult,
-                    ALU.add,
-                )
-            else:
-                copy = nc.scalar.copy if engine == "s" else nc.vector.tensor_copy
-                copy(
-                    dst.rearrange("p (c x i) -> p c i x", x=4, i=PACK),
-                    raw[t, w].rearrange("p i (c x) -> p c i x", x=4),
-                )
-
-        stages = {}
-
-        def round_piece(t, w):
-            for g, pieces in enumerate(GROUPS):
-                if (t, w) in pieces:
-                    if g not in stages:
-                        tag = STAGE_TAG.get(g, f"stage{g}")
-                        shape = [P, len(pieces), P * PACK]
-                        stages[g] = held.tile(shape, BF16, name=f"st{g}", tag=tag, align_bytes=64)
-                    round_weight(stages[g][:, pieces.index((t, w)), :], t, w)
-
-        def quantise(g):
-            pieces = GROUPS[g]
-            group_codes = held.tile([P, len(pieces), P], U32, name=f"codes{g}", align_bytes=64)
-            group_scales = held.tile([P, len(pieces), P], U8, name=f"wscales{g}", align_bytes=64)
+        def quantise(pieces, tag, codes_tag):
+            t0, w0 = pieces[0]
+            stage = held.tile([P, len(pieces), P * PACK], BF16, name=f"st{t0}{w0}", tag=tag, align_bytes=64)
+            for n, (t, w) in enumerate(pieces):
+                if ROUNDERS[t][w] == "g":
+                    nc.gpsimd.tensor_scalar(
+                        stage[:, n, :].rearrange("p (n i) -> p n i", i=PACK),
+                        raw[t, w].rearrange("p i n -> p n i"),
+                        1.0,
+                        0.0,
+                        ALU.mult,
+                        ALU.add,
+                    )
+                else:
+                    copy = nc.scalar.copy if ROUNDERS[t][w] == "s" else nc.vector.tensor_copy
+                    copy(
+                        stage[:, n, :].rearrange("p (c x i) -> p c i x", x=4, i=PACK),
+                        raw[t, w].rearrange("p i (c x) -> p c i x", x=4),
+                    )
+            group_codes = held.tile([P, len(pieces), P], U32, name=f"q{t0}{w0}", tag=codes_tag, align_bytes=64)
+            group_scales = held.tile([P, len(pieces), P], U8, name=f"qs{t0}{w0}", align_bytes=64)
             nc.vector.quantize_mx(
                 out=group_codes[:].rearrange("p w n -> p (w n)").bitcast(FP8X4),
                 scales=group_scales[:].rearrange("p w n -> p (w n)"),
-                in_=stages[g][:].rearrange("p w n -> p (w n)"),
+                in_=stage[:].rearrange("p w n -> p (w n)"),
             )
             for n, piece in enumerate(pieces):
                 codes[piece] = group_codes[:, n, :]
                 scales[piece] = group_scales[:, n, :]
 
-        def quantise_weights(t):
-            for g, pieces in enumerate(GROUPS):
-                if pieces[0][0] == t:
-                    for piece in pieces:
-                        round_piece(*piece)
-                    quantise(g)
-
         made = {}
 
-        def scratch(step, name):
-            if (step, name) in HOLD:
-                made[step, name] = held.tile([P, STEPS[step][2]], F32, name=f"{name}{step}", tag=HOLD[step, name], align_bytes=64)
+        def scratch(step, name, tag=None):
+            if tag is None:
+                made[step, name] = work.tile([P, HALF], F32, name=f"{name}{step}", tag=name)
             else:
-                made[step, name] = work.tile([P, STEPS[step][2]], F32, name=f"{name}{step}", tag=name)
+                made[step, name] = held.tile([P, HALF], F32, name=f"{name}{step}", tag=tag, align_bytes=64)
             return made[step, name]
 
-        def activate(step, name, passes):
-            t, first, width = STEPS[step]
-            h, lo = divmod(first, HALF)
-            acc = psum.tile([P, width], F32, name=f"{name}{step}", tag=name)
+        def by_features(step, name, passes, tag=None):
+            t, h = STEPS[step]
+            acc = psum.tile([P, HALF], F32, name=f"{name}{step}", tag=name)
             for n, (a, w) in enumerate(passes):
                 nc.tensor.matmul_mx(
                     out=acc[:],
                     lhsT=codes[t, w].bitcast(FP8X4),
                     lhsT_scale=scales[t, w],
-                    rhs=picked[a, h][:, lo : lo + width].bitcast(FP8X4),
-                    rhs_scale=picked_scales[a, h][:, lo : lo + width],
+                    rhs=picked[a, h][:].bitcast(FP8X4),
+                    rhs_scale=picked_scales[a, h],
                     start=(n == 0),
                     stop=(n == len(passes) - 1),
                 )
-            act = scratch(step, f"a{name}")
             if name == "z":
-                nc.scalar.activation(act[:], acc[:], ACT.Sigmoid, bias=bias[:, t : t + 1])
+                nc.scalar.activation(scratch(step, "gate", tag)[:], acc[:], ACT.Sigmoid, bias=bias[:, t : t + 1])
             else:
-                nc.scalar.activation(act[:], acc[:], ACT.Tanh)
+                nc.scalar.activation(scratch(step, f"a{name}", tag)[:], acc[:], ACT.Tanh)
 
-        def mix(step):
-            diff = scratch(step, "diff")
-            nc.gpsimd.tensor_tensor(diff[:], made[step, "ahv"][:], made[step, "aht"][:], ALU.subtract)
-            gated = scratch(step, "gated")
-            nc.gpsimd.tensor_tensor(gated[:], diff[:], made[step, "az"][:], ALU.mult)
-
-        def activate_by_entries(step, name, a, w, sign):
-            t, first, width = STEPS[step]
-            h, lo = divmod(first, HALF)
-            acc = psum.tile([P, width // P, P], F32, name=f"{name}{step}", tag=BANK.get((step, name), name))
-            for q in range(width // P):
-                cols = slice(lo + q * P, lo + (q + 1) * P)
+        def by_entries(step, name, a, w, sign, tag=None):
+            t, h = STEPS[step]
+            acc = psum.tile([P, QUARTERS, P], F32, name=f"{name}{step}", tag=name)
+            for q in range(QUARTERS):
                 nc.tensor.matmul_mx(
                     out=acc[:, q, :],
-                    lhsT=picked[a, h][:, cols].bitcast(FP8X4),
-                    lhsT_scale=picked_scales[a, h][:, cols],
+                    lhsT=picked[a, h][:, q * P : (q + 1) * P].bitcast(FP8X4),
+                    lhsT_scale=picked_scales[a, h][:, q * P : (q + 1) * P],
                     rhs=codes[t, w].bitcast(FP8X4),
                     rhs_scale=scales[t, w],
                     start=True,
                     stop=True,
                 )
-            act = scratch(step, f"a{name}")
+            act = scratch(step, f"a{name}", tag)
             nc.scalar.activation(act[:], acc[:].rearrange("p q j -> p (q j)"), ACT.Tanh, scale=sign)
 
-        def turn(step, tag, names):
-            tiles = STEPS[step][2] // P
-            bank = psum.tile([P, tiles, P], F32, name=f"{tag}{step}", tag=f"{tag}{step % 2}")
-            for q in range(tiles):
-                for s, name in enumerate(names):
+        def gate(step, tag=None):
+            by_features(step, "z", ((0, ZV), (1, ZT)), tag)
+
+        def turn(step, bank, names):
+            acc = psum.tile([P, QUARTERS, P], F32, name=f"{bank}{step}", tag=f"{bank}{step % 2}")
+            for q in range(QUARTERS):
+                for n, name in enumerate(names):
                     nc.tensor.matmul(
-                        bank[:, q, :],
+                        acc[:, q, :],
                         made[step, name][:, q * P : (q + 1) * P],
                         ident[:],
-                        start=(s == 0),
-                        stop=(s == len(names) - 1),
+                        start=(n == 0),
+                        stop=(n == len(names) - 1),
                         is_transpose=True,
                     )
-            return bank[:].rearrange("p q j -> p (q j)")
+            return acc[:].rearrange("p q j -> p (q j)")
 
-        def spread_w(h, tag):
-            spread = psum.tile([P, HALF // P, P], F32, name=f"spread{h}", tag=tag)
-            for q in range(HALF // P):
-                col = h * HALF // P + q
+        def gated_on_vector(step):
+            difference = turn(step, "total", ("aht", "ahv"))
+            nc.vector.tensor_tensor(scratch(step, "gated")[:], made[step, "gate"][:], difference, ALU.mult)
+
+        def mixed_on_vector(step):
+            minus_at = turn(step, "back", ("aht",))
+            nc.vector.tensor_tensor(scratch(step, "diff")[:], made[step, "gated"][:], minus_at, ALU.subtract)
+
+        def weighed_on_vector(step, tag=None):
+            h = STEPS[step][1]
+            spread = psum.tile([P, QUARTERS, P], F32, name=f"spread{step}", tag="turned")
+            for q in range(QUARTERS):
+                col = h * QUARTERS + q
                 nc.tensor.transpose(spread[:, q, :], w_cols[:, col : col + 1].to_broadcast([P, P]), ident[:])
-            return spread[:].rearrange("p q j -> p (q j)")
+            result = scratch(step, "result", tag)
+            nc.vector.tensor_tensor(
+                result[:], made[step, "diff"][:], spread[:].rearrange("p q j -> p (q j)"), ALU.mult
+            )
 
-        def mix_short(step):
-            t, first, width = STEPS[step]
-            both = turn(step, "total", ("aht", "ahv"))
-            gated = scratch(step, "gated")
-            nc.vector.tensor_tensor(gated[:], made[step, "az"][:], both, ALU.mult)
+        def gated_on_gpsimd(step, tag=None):
+            by_features(step, "hv", ((0, WV),))
+            by_features(step, "ht", ((1, WT),))
+            gate(step)
+            diff = scratch(step, "diff", tag)
+            nc.gpsimd.tensor_tensor(diff[:], made[step, "ahv"][:], made[step, "aht"][:], ALU.subtract)
+            nc.gpsimd.tensor_tensor(scratch(step, "gated")[:], diff[:], made[step, "gate"][:], ALU.mult)
 
-        def add_short(step):
-            gated = made[step, "gated"]
-            rest = turn(step, "back", ("aht",))
-            mixed = scratch(step, "diff")
-            nc.vector.tensor_tensor(mixed[:], gated[:], rest, ALU.subtract)
-
-        def weigh_short(step):
-            first = STEPS[step][1]
-            result = scratch(step, "result")
-            nc.vector.tensor_tensor(result[:], made[step, "diff"][:], spread_w(first // HALF, "turned"), ALU.mult)
-
-        def add_last(step):
-            result = scratch(step, "result")
-            nc.gpsimd.tensor_tensor(result[:], made[step, "gated"][:], made[step, "aht"][:], ALU.add)
-
-        def weigh(step):
-            t, first, width = STEPS[step]
-            tiles = width // P
-            total = psum.tile([P, tiles, P], F32, name=f"total{step}", tag=f"total{step % 2}")
-            for q in range(tiles):
-                for s, name in enumerate(("gated", "aht")):
-                    nc.tensor.matmul(
-                        total[:, q, :],
-                        made[step, name][:, q * P : (q + 1) * P],
-                        ident[:],
-                        start=(s == 0),
-                        stop=(s == 1),
-                        is_transpose=True,
-                    )
+        def weighed_by_entries(step):
+            h = STEPS[step][1]
+            total = turn(step, "total", ("gated", "aht"))
             weighed = scratch(step, "weighed")
-            for q in range(tiles):
-                col = first // P + q
-                nc.scalar.activation(
-                    weighed[:, q * P : (q + 1) * P],
-                    total[:, q, :],
-                    ACT.Copy,
-                    scale=w_cols[:, col : col + 1],
-                )
-
-        def turn_back(step):
-            tiles = STEPS[step][2] // P
-            weighed = made[step, "weighed"]
-            back = psum.tile([P, tiles, P], F32, name=f"back{step}", tag=f"back{step % 2}")
-            for q in range(tiles):
-                nc.tensor.transpose(back[:, q, :], weighed[:, q * P : (q + 1) * P], ident[:])
-            result = scratch(step, "result")
-            nc.scalar.copy(result[:], back[:].rearrange("p q j -> p (q j)"))
+            for q in range(QUARTERS):
+                col = h * QUARTERS + q
+                cols = slice(q * P, (q + 1) * P)
+                nc.scalar.activation(weighed[:, cols], total[:, cols], ACT.Copy, scale=w_cols[:, col : col + 1])
+            nc.scalar.copy(scratch(step, "result")[:], turn(step, "back", ("weighed",)))
 
         def place(step):
-            t, first, width = STEPS[step]
+            t, h = STEPS[step]
             page = pages[t % PAGES]
-            places = page[:].indirect(lists[0][:, first // 16 : (first + width) // 16])
-            if KINDS[step] == "t":
-                nc.vector.tensor_tensor(places, made[step, "result"][:], w_rows[:, first : first + width], ALU.mult)
+            places = page[:].indirect(lists[0][:, h * LIST_COLS : (h + 1) * LIST_COLS])
+            if step == len(STEPS) - 1:
+                nc.vector.tensor_tensor(places, made[step, "result"][:], w_rows[:], ALU.mult)
             else:
                 nc.vector.tensor_copy(places, made[step, "result"][:])
-            if first + width == J:
+            if h == 1:
                 nc.sync.dma_start(out[t * P : (t + 1) * P, :], page[:])
 
         gather_scales(0, 0, "gs00")
@@ -316,46 +242,43 @@ def tile_list_gmu_tanh_scat_kernel(
         gather_words(0, 0, "gw00")
         gather_scales(1, 0, "gs10")
         gather_words(1, 0, "gw10")
-        gather_words(0, 1, "gw01")
         turned = psum.tile([P, P], F32, tag="turned")
         nc.tensor.transpose(turned[:], small[:], ident[:])
+        columns = held.tile([P, W_ROW + J // P], F32)
         nc.scalar.copy(columns[:], turned[:, 0 : W_ROW + J // P])
-        quantise_weights(0)
-        gather_scales(1, 1, "stage1")
+        bias = columns[:, 0:N_TILES]
+        w_cols = columns[:, W_ROW:]
+        for w in range(4):
+            quantise(((0, w),), f"stage{w}", f"codes{w}")
+        gather_words(0, 1, f"stage{WT}")
         gather_words(1, 1, f"raw{ZT}_0")
-        for tok in """v0 t0 z0 M0 r10 r11 r12 r13 v1 t1 N0 q4 W0 z1 P0 r20 r21 r30 v2 t2 z2 M2 M1 N1 r31 r22 r32 r23 r33 q5 W1 P1 v3 t3 z3 M3 W2 B2 P2 v4 t4 z4 M4 W3 B3 P3 v5 t5 z5 M5 W4 B4 P4 v6 t6 z6 M6 W5 B5 P5 v7 t7 z7 M7 W7 W6 B6 P6 P7""".split():
-            k, step = tok[0], int(tok[1])
-            if k == "v":
-                if KINDS[step] != "v":
-                    activate(step, "hv", ((0, WV),))
-                else:
-                    activate_by_entries(step, "hv", 0, WV, 1.0)
-            elif k == "t":
-                if KINDS[step] != "v":
-                    activate(step, "ht", ((1, WT),))
-                else:
-                    activate_by_entries(step, "ht", 1, WT, -1.0)
-            elif k == "z":
-                activate(step, "z", ((0, ZV), (1, ZT)))
-            elif k == "M":
-                if KINDS[step] != "v":
-                    mix(step)
-                else:
-                    mix_short(step)
-            elif k == "W":
-                if KINDS[step] == "o":
-                    weigh(step)
-                elif KINDS[step] == "t":
-                    add_last(step)
-                else:
-                    weigh_short(step)
-            elif k == "N":
-                add_short(step)
-            elif k == "B":
-                turn_back(step)
-            elif k == "P":
-                place(step)
-            elif k == "r":
-                round_piece(step, int(tok[2]))
-            elif k == "q":
-                quantise(step)
+        gather_scales(1, 1, f"stage{ZT}")
+
+        by_features(0, "hv", ((0, WV),))
+        by_features(0, "ht", ((1, WT),))
+        gate(0, "codes_second")
+        nc.gpsimd.tensor_tensor(scratch(0, "weighed")[:], made[0, "ahv"][:], made[0, "aht"][:], ALU.subtract)
+        nc.vector.tensor_tensor(scratch(0, "gated")[:], made[0, "weighed"][:], made[0, "gate"][:], ALU.mult)
+        quantise(tuple((1, w) for w in range(4)), f"stage{ZV}", "codes_second")
+        nc.vector.tensor_tensor(scratch(0, "diff")[:], made[0, "gated"][:], made[0, "aht"][:], ALU.add)
+        by_entries(1, "hv", 0, WV, 1.0)
+        by_entries(1, "ht", 1, WT, -1.0)
+        weighed_on_vector(0)
+        gate(1)
+        place(0)
+        gated_on_vector(1)
+        gated_on_gpsimd(2)
+        mixed_on_vector(1)
+        quantise(tuple((t, w) for w in range(4) for t in (2, 3)), f"stage{ZV}", "codes_late")
+        weighed_on_vector(1, f"raw{ZT}_2")
+        place(1)
+        last = len(STEPS) - 1
+        for step in range(3, last + 1):
+            gated_on_gpsimd(step, f"stage{ZV}" if step == 3 else None)
+            if step == last:
+                nc.gpsimd.tensor_tensor(
+                    scratch(step, "result")[:], made[step, "gated"][:], made[step, "aht"][:], ALU.add
+                )
+            weighed_by_entries(step - 1)
+            place(step - 1)
+        place(last)

@@ -41,10 +41,6 @@ def tile_list_gmu_tanh_scat_kernel(
         work = ctx.enter_context(tc.tile_pool(name="work", bufs=3))
         psum = ctx.enter_context(tc.psum_pool(name="psum", bufs=1))
 
-        warm = held.tile([P, 2], F32)
-        nc.vector.memset(warm[:, 0:1], 0.0)
-        nc.scalar.activation(warm[:, 1:2], warm[:, 0:1], ACT.Sigmoid)
-
         lists = [held.tile([P, J // 16], U16, name=f"list{a}") for a in range(2)]
         words = [held.tile([P, T], I32, name=f"words{a}") for a in range(2)]
         planes = [held.tile([P, T], U8, name=f"plane{a}") for a in range(2)]

@@ -26,9 +26,10 @@ WV, WT, ZV, ZT = range(4)
 BLOCKS = ((0, 1), (1, 2), (2, 4))
 W_ROW = 8
 PLANE_ROW = (0, 4)
-PAGES = 2
-STEPS = tuple((t, h) for t in range(N_TILES) for h in range(2))
-ROUNDERS = ("ssss", "ssvv", "ggss", "ssss")
+FIRST_ZEROED = 1280
+PAGE_OF = (0, 1, 0, 2)
+STEPS = ((0, 0), (0, 1), (1, 0), (1, 1), (2, 0), (3, 0), (2, 1), (3, 1))
+ROUNDERS = ("ssss", "ssgg", "ggss", "ssss")
 
 
 def tile_list_gmu_tanh_scat_kernel(
@@ -42,12 +43,14 @@ def tile_list_gmu_tanh_scat_kernel(
         psum = ctx.enter_context(tc.psum_pool(name="psum", bufs=1))
 
         lists = [held.tile([P, J // 16], U16, name=f"list{a}") for a in range(2)]
-        words = [held.tile([P, T], I32, name=f"words{a}") for a in range(2)]
+        words = [held.tile([P, T], I32, name=f"words{a}", align_bytes=64) for a in range(2)]
         planes = [held.tile([P, T], U8, name=f"plane{a}") for a in range(2)]
-        for plane in planes:
-            nc.gpsimd.memset(plane[:].bitcast(I32), 0)
-        small = held.tile([P, P], F32)
-        nc.gpsimd.memset(small[:], 0.0)
+        small = held.tile([P, P], F32, tag="small")
+        ident = held.tile([P, P], F32)
+        pages = [held.tile([P, T], F32, name=f"page{g}") for g in range(2)]
+        for zeroed in (planes[0], ident, planes[1], small, *pages):
+            nc.vector.memset(zeroed[:].bitcast(I32), 0)
+        make_identity(nc, ident[:], nomemset=True)
 
         def load_table(a, table_words, table_scales):
             rows = table_scales[0].rearrange("(q r) t -> r q t", r=4)
@@ -64,18 +67,18 @@ def tile_list_gmu_tanh_scat_kernel(
         raw = {}
         for t0, t1 in BLOCKS:
             for w in range(4):
-                block = held.tile([P, PACK, (t1 - t0) * P], F32, name=f"raw{w}_{t0}", align_bytes=64)
-                nc.sync.dma_start(block[:], weights[w].rearrange("(p i) n -> p i n", i=PACK)[:, :, t0 * P : t1 * P])
-                for t in range(t0, t1):
-                    raw[t, w] = block[:, :, (t - t0) * P : (t - t0 + 1) * P]
-        w_rows = held.tile([P, HALF], F32)
-        nc.sync.dma_start(w_rows[:], wgo[:, STEPS[-1][1] * HALF : (STEPS[-1][1] + 1) * HALF])
+                width = 1 if w == ZT else t1 - t0
+                for first in range(t0, t1, width):
+                    block = held.tile([P, PACK, width * P], F32, name=f"raw{w}_{first}", align_bytes=64)
+                    nc.sync.dma_start(
+                        block[:], weights[w].rearrange("(p i) n -> p i n", i=PACK)[:, :, first * P : (first + width) * P]
+                    )
+                    for t in range(first, first + width):
+                        raw[t, w] = block[:, :, (t - first) * P : (t - first + 1) * P]
 
-        ident = held.tile([P, P], F32)
-        make_identity(nc, ident[:])
-        pages = [held.tile([P, T], F32, name=f"page{g}") for g in range(PAGES)]
-        for page in pages:
-            nc.vector.memset(page[:].bitcast(I32), 0)
+
+        warm = held.tile([P, 1], F32)
+        nc.scalar.activation(warm[:], ident[:, 0:1], ACT.Sigmoid)
 
         picked = {}
         picked_scales = {}
@@ -95,7 +98,7 @@ def tile_list_gmu_tanh_scat_kernel(
         codes = {}
         scales = {}
 
-        def quantise(pieces, tag, codes_tag):
+        def round_pieces(pieces, tag):
             t0, w0 = pieces[0]
             stage = held.tile([P, len(pieces), P * PACK], BF16, name=f"st{t0}{w0}", tag=tag, align_bytes=64)
             for n, (t, w) in enumerate(pieces):
@@ -114,12 +117,16 @@ def tile_list_gmu_tanh_scat_kernel(
                         stage[:, n, :].rearrange("p (c x i) -> p c i x", x=4, i=PACK),
                         raw[t, w].rearrange("p i (c x) -> p c i x", x=4),
                     )
+            return stage[:]
+
+        def quantise(pieces, codes_tag, stage):
+            t0, w0 = pieces[0]
             group_codes = held.tile([P, len(pieces), P], U32, name=f"q{t0}{w0}", tag=codes_tag, align_bytes=64)
             group_scales = held.tile([P, len(pieces), P], U8, name=f"qs{t0}{w0}", align_bytes=64)
             nc.vector.quantize_mx(
                 out=group_codes[:].rearrange("p w n -> p (w n)").bitcast(FP8X4),
                 scales=group_scales[:].rearrange("p w n -> p (w n)"),
-                in_=stage[:].rearrange("p w n -> p (w n)"),
+                in_=stage.rearrange("p w n -> p (w n)"),
             )
             for n, piece in enumerate(pieces):
                 codes[piece] = group_codes[:, n, :]
@@ -152,9 +159,9 @@ def tile_list_gmu_tanh_scat_kernel(
             else:
                 nc.scalar.activation(scratch(step, f"a{name}", tag)[:], acc[:], ACT.Tanh)
 
-        def by_entries(step, name, a, w, sign, tag=None):
+        def by_entries(step, name, a, w, sign, tag=None, bank=None):
             t, h = STEPS[step]
-            acc = psum.tile([P, QUARTERS, P], F32, name=f"{name}{step}", tag=name)
+            acc = psum.tile([P, QUARTERS, P], F32, name=f"{name}{step}", tag=bank or name)
             for q in range(QUARTERS):
                 nc.tensor.matmul_mx(
                     out=acc[:, q, :],
@@ -167,6 +174,31 @@ def tile_list_gmu_tanh_scat_kernel(
                 )
             act = scratch(step, f"a{name}", tag)
             nc.scalar.activation(act[:], acc[:].rearrange("p q j -> p (q j)"), ACT.Tanh, scale=sign)
+
+        def weigh_entries(step, name):
+            h = STEPS[step][1]
+            weighed = scratch(step, f"w{name}")
+            for q in range(QUARTERS):
+                col = h * QUARTERS + q
+                cols = slice(q * P, (q + 1) * P)
+                nc.scalar.activation(
+                    weighed[:, cols], made[step, name][:, cols], ACT.Copy, scale=w_cols[:, col : col + 1]
+                )
+
+        def add_turned(acc, source, first, last):
+            for q in range(QUARTERS):
+                nc.tensor.matmul(
+                    acc[:, q, :],
+                    source[:, q * P : (q + 1) * P],
+                    ident[:],
+                    start=(first and q == 0),
+                    stop=(last and q == QUARTERS - 1),
+                    is_transpose=True,
+                )
+
+        def on_vector(target, left, right, op):
+            for cols in (slice(0, HALF // 2), slice(HALF // 2, HALF)):
+                nc.vector.tensor_tensor(target[:, cols], left[:, cols], right[:, cols], op)
 
         def gate(step, tag=None):
             by_features(step, "z", ((0, ZV), (1, ZT)), tag)
@@ -187,11 +219,11 @@ def tile_list_gmu_tanh_scat_kernel(
 
         def gated_on_vector(step):
             difference = turn(step, "total", ("aht", "ahv"))
-            nc.vector.tensor_tensor(scratch(step, "gated")[:], made[step, "gate"][:], difference, ALU.mult)
+            on_vector(scratch(step, "gated"), made[step, "gate"], difference, ALU.mult)
 
         def mixed_on_vector(step):
             minus_at = turn(step, "back", ("aht",))
-            nc.vector.tensor_tensor(scratch(step, "diff")[:], made[step, "gated"][:], minus_at, ALU.subtract)
+            on_vector(scratch(step, "diff"), made[step, "gated"], minus_at, ALU.subtract)
 
         def weighed_on_vector(step, tag=None):
             h = STEPS[step][1]
@@ -215,7 +247,7 @@ def tile_list_gmu_tanh_scat_kernel(
         def weighed_by_entries(step):
             h = STEPS[step][1]
             total = turn(step, "total", ("gated", "aht"))
-            weighed = scratch(step, "weighed")
+            weighed = scratch(step, "weighed", "w_rows" if step == len(STEPS) - 2 else None)
             for q in range(QUARTERS):
                 col = h * QUARTERS + q
                 cols = slice(q * P, (q + 1) * P)
@@ -224,7 +256,7 @@ def tile_list_gmu_tanh_scat_kernel(
 
         def place(step):
             t, h = STEPS[step]
-            page = pages[t % PAGES]
+            page = pages[PAGE_OF[t]]
             places = page[:].indirect(lists[0][:, h * LIST_COLS : (h + 1) * LIST_COLS])
             if step == len(STEPS) - 1:
                 nc.vector.tensor_tensor(places, made[step, "result"][:], w_rows[:], ALU.mult)
@@ -242,39 +274,53 @@ def tile_list_gmu_tanh_scat_kernel(
         nc.tensor.transpose(turned[:], small[:], ident[:])
         columns = held.tile([P, W_ROW + J // P], F32)
         nc.scalar.copy(columns[:], turned[:, 0 : W_ROW + J // P])
+        pages.append(held.tile([P, T], F32, name="page2", tag="small"))
         bias = columns[:, 0:N_TILES]
         w_cols = columns[:, W_ROW:]
         for w in range(4):
-            quantise(((0, w),), f"stage{w}", f"codes{w}")
-        gather_words(0, 1, f"stage{WT}")
-        gather_words(1, 1, f"raw{ZT}_0")
-        gather_scales(1, 1, f"stage{ZT}")
+            quantise(((0, w),), f"codes{w}", round_pieces(((0, w),), f"stage{w}"))
+        for cols in (slice(0, FIRST_ZEROED), slice(FIRST_ZEROED, T)):
+            nc.vector.memset(pages[2][:, cols].bitcast(I32), 0)
+        gather_words(0, 1, f"raw{WT}_0")
+        gather_scales(1, 1, f"raw{ZT}_0")
+        gather_words(1, 1, f"stage{ZT}")
 
-        by_features(0, "hv", ((0, WV),))
-        by_features(0, "ht", ((1, WT),))
+        by_entries(0, "hv", 0, WV, 1.0)
+        weigh_entries(0, "ahv")
+        by_entries(0, "ht", 1, WT, -1.0)
+        weigh_entries(0, "aht")
         gate(0, "codes_second")
-        nc.gpsimd.tensor_tensor(scratch(0, "weighed")[:], made[0, "ahv"][:], made[0, "aht"][:], ALU.subtract)
-        nc.vector.tensor_tensor(scratch(0, "gated")[:], made[0, "weighed"][:], made[0, "gate"][:], ALU.mult)
-        quantise(tuple((1, w) for w in range(4)), f"stage{ZV}", "codes_second")
-        nc.vector.tensor_tensor(scratch(0, "diff")[:], made[0, "gated"][:], made[0, "aht"][:], ALU.add)
+        first_difference = psum.tile([P, QUARTERS, P], F32, tag="total0")
+        add_turned(first_difference, made[0, "wahv"], True, False)
+        add_turned(first_difference, made[0, "waht"], False, True)
+        on_vector(scratch(0, "gated", "codes_third"), made[0, "gate"], first_difference[:].rearrange("p q j -> p (q j)"), ALU.mult)
+        minus_at = turn(0, "back", ("waht",))
+        second = tuple((1, w) for w in range(4))
+        quantise(second[:2], "codes_second", round_pieces(second[:2], "stage_second"))
+        on_vector(scratch(0, "result"), made[0, "gated"], minus_at, ALU.subtract)
+        quantise(second[2:], "codes_third", round_pieces(second[2:], "words1"))
         by_entries(1, "hv", 0, WV, 1.0)
-        by_entries(1, "ht", 1, WT, -1.0)
-        weighed_on_vector(0)
+        by_entries(1, "ht", 1, WT, -1.0, bank="total0")
         gate(1)
         place(0)
         gated_on_vector(1)
         gated_on_gpsimd(2)
         mixed_on_vector(1)
-        quantise(tuple((t, w) for w in range(4) for t in (2, 3)), f"stage{ZV}", "codes_late")
+        late = tuple((t, w) for w in range(4) for t in (2, 3))
+        late_stage = round_pieces(late, "words1")
         weighed_on_vector(1, f"raw{ZT}_2")
+        quantise(late, "codes_late", late_stage)
         place(1)
         last = len(STEPS) - 1
         for step in range(3, last + 1):
-            gated_on_gpsimd(step, f"stage{ZV}" if step == 3 else None)
+            gated_on_gpsimd(step, "words1" if step == 3 else None)
             if step == last:
                 nc.gpsimd.tensor_tensor(
                     scratch(step, "result")[:], made[step, "gated"][:], made[step, "aht"][:], ALU.add
                 )
             weighed_by_entries(step - 1)
+            if step == last:
+                w_rows = held.tile([P, HALF], F32, tag="w_rows", align_bytes=64)
+                nc.sync.dma_start(w_rows[:], wgo[:, STEPS[last][1] * HALF : (STEPS[last][1] + 1) * HALF])
             place(step - 1)
         place(last)

@@ -27,8 +27,9 @@ BLOCKS = ((0, 1), (1, 2), (2, 4))
 W_ROW = 8
 PLANE_ROW = (0, 4)
 FIRST_ZEROED = 1280
-PAGE_OF = (0, 1, 0, 2)
-STEPS = ((0, 0), (0, 1), (1, 0), (1, 1), (2, 0), (3, 0), (2, 1), (3, 1))
+AT_RAW_ZT = 0
+PAGE_OF = (0, 1, 2, 0)
+STEPS = ((0, 0), (1, 0), (0, 1), (1, 1), (2, 0), (3, 0), (2, 1), (3, 1))
 ROUNDERS = ("ssss", "ssgg", "ggss", "ssss")
 
 
@@ -41,6 +42,7 @@ def tile_list_gmu_tanh_scat_kernel(
         held = ctx.enter_context(tc.tile_pool(name="held", bufs=1))
         work = ctx.enter_context(tc.tile_pool(name="work", bufs=3))
         psum = ctx.enter_context(tc.psum_pool(name="psum", bufs=1))
+        turns = ctx.enter_context(tc.tile_pool(name="turns", bufs=1))
 
         lists = [held.tile([P, J // 16], U16, name=f"list{a}") for a in range(2)]
         words = [held.tile([P, T], I32, name=f"words{a}", align_bytes=64) for a in range(2)]
@@ -51,6 +53,11 @@ def tile_list_gmu_tanh_scat_kernel(
         for zeroed in (planes[0], ident, planes[1], small, *pages):
             nc.vector.memset(zeroed[:].bitcast(I32), 0)
         make_identity(nc, ident[:], nomemset=True)
+
+        def placed(shape, dtype, name, where):
+            if isinstance(where, int):
+                return turns.tile(shape, dtype, name=name, offset=where, align_bytes=64)
+            return held.tile(shape, dtype, name=name, tag=where or name, align_bytes=64)
 
         def load_table(a, table_words, table_scales):
             rows = table_scales[0].rearrange("(q r) t -> r q t", r=4)
@@ -69,7 +76,8 @@ def tile_list_gmu_tanh_scat_kernel(
             for w in range(4):
                 width = 1 if w == ZT else t1 - t0
                 for first in range(t0, t1, width):
-                    block = held.tile([P, PACK, width * P], F32, name=f"raw{w}_{first}", align_bytes=64)
+                    where = AT_RAW_ZT if (first, w) == (0, ZT) else None
+                    block = placed([P, PACK, width * P], F32, f"raw{w}_{first}", where)
                     nc.sync.dma_start(
                         block[:], weights[w].rearrange("(p i) n -> p i n", i=PACK)[:, :, first * P : (first + width) * P]
                     )
@@ -90,7 +98,7 @@ def tile_list_gmu_tanh_scat_kernel(
             picked[a, h] = tile
 
         def gather_scales(a, h, tag):
-            tile = held.tile([P, HALF], U8, name=f"gs{a}{h}", tag=tag, align_bytes=64)
+            tile = placed([P, HALF], U8, f"gs{a}{h}", tag)
             entries = lists[a][:, h * LIST_COLS : (h + 1) * LIST_COLS]
             nc.vector.tensor_copy(tile[:], planes[a][:].indirect(entries))
             picked_scales[a, h] = tile[PLANE_ROW[a] : P, :]
@@ -138,12 +146,12 @@ def tile_list_gmu_tanh_scat_kernel(
             if tag is None:
                 made[step, name] = work.tile([P, HALF], F32, name=f"{name}{step}", tag=name)
             else:
-                made[step, name] = held.tile([P, HALF], F32, name=f"{name}{step}", tag=tag, align_bytes=64)
+                made[step, name] = placed([P, HALF], F32, f"{name}{step}", tag)
             return made[step, name]
 
-        def by_features(step, name, passes, tag=None):
+        def by_features(step, name, passes, tag=None, bank=None):
             t, h = STEPS[step]
-            acc = psum.tile([P, HALF], F32, name=f"{name}{step}", tag=name)
+            acc = psum.tile([P, HALF], F32, name=f"{name}{step}", tag=bank or name)
             for n, (a, w) in enumerate(passes):
                 nc.tensor.matmul_mx(
                     out=acc[:],
@@ -236,9 +244,9 @@ def tile_list_gmu_tanh_scat_kernel(
                 result[:], made[step, "diff"][:], spread[:].rearrange("p q j -> p (q j)"), ALU.mult
             )
 
-        def gated_on_gpsimd(step, tag=None):
+        def gated_on_gpsimd(step, tag=None, bank=None):
             by_features(step, "hv", ((0, WV),))
-            by_features(step, "ht", ((1, WT),))
+            by_features(step, "ht", ((1, WT),), bank=bank)
             gate(step)
             diff = scratch(step, "diff", tag)
             nc.gpsimd.tensor_tensor(diff[:], made[step, "ahv"][:], made[step, "aht"][:], ALU.subtract)
@@ -282,10 +290,10 @@ def tile_list_gmu_tanh_scat_kernel(
         for cols in (slice(0, FIRST_ZEROED), slice(FIRST_ZEROED, T)):
             nc.vector.memset(pages[2][:, cols].bitcast(I32), 0)
         gather_words(0, 1, f"raw{WT}_0")
-        gather_scales(1, 1, f"raw{ZT}_0")
+        gather_scales(1, 1, AT_RAW_ZT)
         gather_words(1, 1, f"stage{ZT}")
 
-        by_entries(0, "hv", 0, WV, 1.0)
+        by_entries(0, "hv", 0, WV, 1.0, AT_RAW_ZT + HALF)
         weigh_entries(0, "ahv")
         by_entries(0, "ht", 1, WT, -1.0)
         weigh_entries(0, "aht")
@@ -299,12 +307,12 @@ def tile_list_gmu_tanh_scat_kernel(
         quantise(second[:2], "codes_second", round_pieces(second[:2], "stage_second"))
         on_vector(scratch(0, "result"), made[0, "gated"], minus_at, ALU.subtract)
         quantise(second[2:], "codes_third", round_pieces(second[2:], "words1"))
+        gated_on_gpsimd(2, bank="total0")
         by_entries(1, "hv", 0, WV, 1.0)
-        by_entries(1, "ht", 1, WT, -1.0, bank="total0")
+        by_entries(1, "ht", 1, WT, -1.0)
         gate(1)
         place(0)
         gated_on_vector(1)
-        gated_on_gpsimd(2)
         mixed_on_vector(1)
         late = tuple((t, w) for w in range(4) for t in (2, 3))
         late_stage = round_pieces(late, "words1")

@@ -28,9 +28,10 @@ W_ROW = 8
 PLANE_ROW = (0, 4)
 FIRST_ZEROED = 1280
 AT_RAW_ZT = 0
+AT_STAGE_ZT = 6144
 PAGE_OF = (0, 1, 2, 0)
 STEPS = ((0, 0), (1, 0), (0, 1), (1, 1), (2, 0), (3, 0), (2, 1), (3, 1))
-ROUNDERS = ("ssss", "ssgg", "ggss", "ssss")
+ROUNDERS = ("ssss", "gggs", "ggss", "gsss")
 
 
 def tile_list_gmu_tanh_scat_kernel(
@@ -92,7 +93,7 @@ def tile_list_gmu_tanh_scat_kernel(
         picked_scales = {}
 
         def gather_words(a, h, tag):
-            tile = held.tile([P, HALF], U32, name=f"gw{a}{h}", tag=tag, align_bytes=64)
+            tile = placed([P, HALF], U32, f"gw{a}{h}", tag)
             entries = lists[a][:, h * LIST_COLS : (h + 1) * LIST_COLS]
             nc.vector.tensor_copy(tile[:], words[a][:].bitcast(U32).indirect(entries))
             picked[a, h] = tile
@@ -106,10 +107,11 @@ def tile_list_gmu_tanh_scat_kernel(
         codes = {}
         scales = {}
 
-        def round_pieces(pieces, tag):
+        def round_pieces(pieces, tag, order=None):
             t0, w0 = pieces[0]
-            stage = held.tile([P, len(pieces), P * PACK], BF16, name=f"st{t0}{w0}", tag=tag, align_bytes=64)
-            for n, (t, w) in enumerate(pieces):
+            stage = placed([P, len(pieces), P * PACK], BF16, f"st{t0}{w0}", tag)
+            for n in order or range(len(pieces)):
+                t, w = pieces[n]
                 if ROUNDERS[t][w] == "g":
                     nc.gpsimd.tensor_scalar(
                         stage[:, n, :].rearrange("p (n i) -> p n i", i=PACK),
@@ -129,7 +131,7 @@ def tile_list_gmu_tanh_scat_kernel(
 
         def quantise(pieces, codes_tag, stage):
             t0, w0 = pieces[0]
-            group_codes = held.tile([P, len(pieces), P], U32, name=f"q{t0}{w0}", tag=codes_tag, align_bytes=64)
+            group_codes = placed([P, len(pieces), P], U32, f"q{t0}{w0}", codes_tag)
             group_scales = held.tile([P, len(pieces), P], U8, name=f"qs{t0}{w0}", align_bytes=64)
             nc.vector.quantize_mx(
                 out=group_codes[:].rearrange("p w n -> p (w n)").bitcast(FP8X4),
@@ -183,9 +185,9 @@ def tile_list_gmu_tanh_scat_kernel(
             act = scratch(step, f"a{name}", tag)
             nc.scalar.activation(act[:], acc[:].rearrange("p q j -> p (q j)"), ACT.Tanh, scale=sign)
 
-        def weigh_entries(step, name):
+        def weigh_entries(step, name, tag=None):
             h = STEPS[step][1]
-            weighed = scratch(step, f"w{name}")
+            weighed = scratch(step, f"w{name}", tag)
             for q in range(QUARTERS):
                 col = h * QUARTERS + q
                 cols = slice(q * P, (q + 1) * P)
@@ -208,8 +210,8 @@ def tile_list_gmu_tanh_scat_kernel(
             for cols in (slice(0, HALF // 2), slice(HALF // 2, HALF)):
                 nc.vector.tensor_tensor(target[:, cols], left[:, cols], right[:, cols], op)
 
-        def gate(step, tag=None):
-            by_features(step, "z", ((0, ZV), (1, ZT)), tag)
+        def gate(step, bank=None):
+            by_features(step, "z", ((0, ZV), (1, ZT)), None, bank)
 
         def turn(step, bank, names):
             acc = psum.tile([P, QUARTERS, P], F32, name=f"{bank}{step}", tag=f"{bank}{step % 2}")
@@ -231,7 +233,7 @@ def tile_list_gmu_tanh_scat_kernel(
 
         def mixed_on_vector(step):
             minus_at = turn(step, "back", ("aht",))
-            on_vector(scratch(step, "diff"), made[step, "gated"], minus_at, ALU.subtract)
+            on_vector(scratch(step, "diff", "codes_late"), made[step, "gated"], minus_at, ALU.subtract)
 
         def weighed_on_vector(step, tag=None):
             h = STEPS[step][1]
@@ -244,13 +246,15 @@ def tile_list_gmu_tanh_scat_kernel(
                 result[:], made[step, "diff"][:], spread[:].rearrange("p q j -> p (q j)"), ALU.mult
             )
 
-        def gated_on_gpsimd(step, tag=None, bank=None):
+        def difference_on_gpsimd(step, tag=None, bank=None):
             by_features(step, "hv", ((0, WV),))
             by_features(step, "ht", ((1, WT),), bank=bank)
-            gate(step)
             diff = scratch(step, "diff", tag)
             nc.gpsimd.tensor_tensor(diff[:], made[step, "ahv"][:], made[step, "aht"][:], ALU.subtract)
-            nc.gpsimd.tensor_tensor(scratch(step, "gated")[:], diff[:], made[step, "gate"][:], ALU.mult)
+
+        def gated_on_gpsimd(step, bank=None):
+            gate(step, bank)
+            nc.gpsimd.tensor_tensor(scratch(step, "gated")[:], made[step, "diff"][:], made[step, "gate"][:], ALU.mult)
 
         def weighed_by_entries(step):
             h = STEPS[step][1]
@@ -286,42 +290,48 @@ def tile_list_gmu_tanh_scat_kernel(
         bias = columns[:, 0:N_TILES]
         w_cols = columns[:, W_ROW:]
         for w in range(4):
-            quantise(((0, w),), f"codes{w}", round_pieces(((0, w),), f"stage{w}"))
+            quantise(((0, w),), f"codes{w}", round_pieces(((0, w),), AT_STAGE_ZT if w == ZT else f"stage{w}"))
         for cols in (slice(0, FIRST_ZEROED), slice(FIRST_ZEROED, T)):
             nc.vector.memset(pages[2][:, cols].bitcast(I32), 0)
         gather_words(0, 1, f"raw{WT}_0")
         gather_scales(1, 1, AT_RAW_ZT)
-        gather_words(1, 1, f"stage{ZT}")
+        gather_words(1, 1, AT_STAGE_ZT - 3 * HALF)
+        second = tuple((1, w) for w in range(4))
+        quantise(second[:2], None, round_pieces(second[:2], AT_STAGE_ZT + HALF))
 
         by_entries(0, "hv", 0, WV, 1.0, AT_RAW_ZT + HALF)
         weigh_entries(0, "ahv")
         by_entries(0, "ht", 1, WT, -1.0)
-        weigh_entries(0, "aht")
-        gate(0, "codes_second")
+        weigh_entries(0, "aht", "late_stage")
+        gate(0)
         first_difference = psum.tile([P, QUARTERS, P], F32, tag="total0")
         add_turned(first_difference, made[0, "wahv"], True, False)
         add_turned(first_difference, made[0, "waht"], False, True)
         on_vector(scratch(0, "gated", "codes_third"), made[0, "gate"], first_difference[:].rearrange("p q j -> p (q j)"), ALU.mult)
         minus_at = turn(0, "back", ("waht",))
-        second = tuple((1, w) for w in range(4))
-        quantise(second[:2], "codes_second", round_pieces(second[:2], "stage_second"))
         on_vector(scratch(0, "result"), made[0, "gated"], minus_at, ALU.subtract)
-        quantise(second[2:], "codes_third", round_pieces(second[2:], "words1"))
-        gated_on_gpsimd(2, bank="total0")
-        by_entries(1, "hv", 0, WV, 1.0)
-        by_entries(1, "ht", 1, WT, -1.0)
-        gate(1)
+        quantise(second[2:], "codes_third", round_pieces(second[2:], AT_STAGE_ZT + HALF))
+        difference_on_gpsimd(2, bank="z")
+        by_entries(1, "hv", 0, WV, 1.0, bank="total0")
+        by_entries(1, "ht", 1, WT, -1.0, bank="z")
+        gated_on_gpsimd(2, "total0")
+        gate(1, "ht")
         place(0)
         gated_on_vector(1)
         mixed_on_vector(1)
-        late = tuple((t, w) for w in range(4) for t in (2, 3))
-        late_stage = round_pieces(late, "words1")
+        by_gpsimd = ((2, WV), (3, WV), (2, WT))
+        by_scalar = ((2, ZT), (3, WT), (2, ZV), (3, ZV), (3, ZT))
+        gpsimd_stage = round_pieces(by_gpsimd, AT_STAGE_ZT + HALF)
+        scalar_stage = round_pieces(by_scalar, "late_stage", (1, 2, 3, 0, 4))
         weighed_on_vector(1, f"raw{ZT}_2")
-        quantise(late, "codes_late", late_stage)
+        quantise(by_gpsimd, "codes_late", gpsimd_stage)
+        quantise(by_scalar[:1], None, scalar_stage[:, :1, :])
+        quantise(by_scalar[1:], None, scalar_stage[:, 1:, :])
         place(1)
         last = len(STEPS) - 1
         for step in range(3, last + 1):
-            gated_on_gpsimd(step, "words1" if step == 3 else None)
+            difference_on_gpsimd(step, "late_stage" if step == 3 else None)
+            gated_on_gpsimd(step)
             if step == last:
                 nc.gpsimd.tensor_tensor(
                     scratch(step, "result")[:], made[step, "gated"][:], made[step, "aht"][:], ALU.add

@@ -29,9 +29,10 @@ PLANE_ROW = (0, 4)
 FIRST_ZEROED = 1280
 AT_RAW_ZT = 0
 AT_STAGE_ZT = 6144
+AT_MIXED = 10240
 PAGE_OF = (0, 1, 2, 0)
 STEPS = ((0, 0), (1, 0), (0, 1), (1, 1), (2, 0), (3, 0), (2, 1), (3, 1))
-ROUNDERS = ("ssss", "gggs", "ggss", "gsss")
+ROUNDERS = ("ssss", "vvss", "gggs", "sgss")
 
 
 def tile_list_gmu_tanh_scat_kernel(
@@ -107,10 +108,14 @@ def tile_list_gmu_tanh_scat_kernel(
         codes = {}
         scales = {}
 
-        def round_pieces(pieces, tag, order=None):
+        def round_pieces(pieces, tag, chosen=None):
             t0, w0 = pieces[0]
             stage = placed([P, len(pieces), P * PACK], BF16, f"st{t0}{w0}", tag)
-            for n in order or range(len(pieces)):
+            round_into(stage, pieces, chosen or range(len(pieces)))
+            return stage[:]
+
+        def round_into(stage, pieces, chosen):
+            for n in chosen:
                 t, w = pieces[n]
                 if ROUNDERS[t][w] == "g":
                     nc.gpsimd.tensor_scalar(
@@ -127,7 +132,6 @@ def tile_list_gmu_tanh_scat_kernel(
                         stage[:, n, :].rearrange("p (c x i) -> p c i x", x=4, i=PACK),
                         raw[t, w].rearrange("p i (c x) -> p c i x", x=4),
                     )
-            return stage[:]
 
         def quantise(pieces, codes_tag, stage):
             t0, w0 = pieces[0]
@@ -183,7 +187,11 @@ def tile_list_gmu_tanh_scat_kernel(
                     stop=True,
                 )
             act = scratch(step, f"a{name}", tag)
-            nc.scalar.activation(act[:], acc[:].rearrange("p q j -> p (q j)"), ACT.Tanh, scale=sign)
+            flat = acc[:].rearrange("p q j -> p (q j)")
+            parts = 2 if step == 0 else 1
+            for part in range(parts):
+                cols = slice(part * HALF // parts, (part + 1) * HALF // parts)
+                nc.scalar.activation(act[:, cols], flat[:, cols], ACT.Tanh, scale=sign)
 
         def weigh_entries(step, name, tag=None):
             h = STEPS[step][1]
@@ -210,11 +218,12 @@ def tile_list_gmu_tanh_scat_kernel(
             for cols in (slice(0, HALF // 2), slice(HALF // 2, HALF)):
                 nc.vector.tensor_tensor(target[:, cols], left[:, cols], right[:, cols], op)
 
-        def gate(step, bank=None):
-            by_features(step, "z", ((0, ZV), (1, ZT)), None, bank)
+        def gate(step, bank=None, tag=None):
+            by_features(step, "z", ((0, ZV), (1, ZT)), tag, bank)
 
         def turn(step, bank, names):
-            acc = psum.tile([P, QUARTERS, P], F32, name=f"{bank}{step}", tag=f"{bank}{step % 2}")
+            turn_of_bank = 1 if bank == "total" and step >= 3 else step % 2
+            acc = psum.tile([P, QUARTERS, P], F32, name=f"{bank}{step}", tag=f"{bank}{turn_of_bank}")
             for q in range(QUARTERS):
                 for n, name in enumerate(names):
                     nc.tensor.matmul(
@@ -233,7 +242,7 @@ def tile_list_gmu_tanh_scat_kernel(
 
         def mixed_on_vector(step):
             minus_at = turn(step, "back", ("aht",))
-            on_vector(scratch(step, "diff", "codes_late"), made[step, "gated"], minus_at, ALU.subtract)
+            on_vector(scratch(step, "diff", AT_MIXED), made[step, "gated"], minus_at, ALU.subtract)
 
         def weighed_on_vector(step, tag=None):
             h = STEPS[step][1]
@@ -241,10 +250,7 @@ def tile_list_gmu_tanh_scat_kernel(
             for q in range(QUARTERS):
                 col = h * QUARTERS + q
                 nc.tensor.transpose(spread[:, q, :], w_cols[:, col : col + 1].to_broadcast([P, P]), ident[:])
-            result = scratch(step, "result", tag)
-            nc.vector.tensor_tensor(
-                result[:], made[step, "diff"][:], spread[:].rearrange("p q j -> p (q j)"), ALU.mult
-            )
+            on_vector(scratch(step, "result", tag), made[step, "diff"], spread[:].rearrange("p q j -> p (q j)"), ALU.mult)
 
         def difference_on_gpsimd(step, tag=None, bank=None):
             by_features(step, "hv", ((0, WV),))
@@ -297,41 +303,43 @@ def tile_list_gmu_tanh_scat_kernel(
         gather_scales(1, 1, AT_RAW_ZT)
         gather_words(1, 1, AT_STAGE_ZT - 3 * HALF)
         second = tuple((1, w) for w in range(4))
-        quantise(second[:2], None, round_pieces(second[:2], AT_STAGE_ZT + HALF))
+        second_stage = round_pieces(second[:2], AT_STAGE_ZT + HALF)
 
         by_entries(0, "hv", 0, WV, 1.0, AT_RAW_ZT + HALF)
         weigh_entries(0, "ahv")
         by_entries(0, "ht", 1, WT, -1.0)
         weigh_entries(0, "aht", "late_stage")
-        gate(0)
+        gate(0, tag="codes_second")
+        third_stage = round_pieces(second[2:], AT_RAW_ZT + HALF)
         first_difference = psum.tile([P, QUARTERS, P], F32, tag="total0")
         add_turned(first_difference, made[0, "wahv"], True, False)
         add_turned(first_difference, made[0, "waht"], False, True)
         on_vector(scratch(0, "gated", "codes_third"), made[0, "gate"], first_difference[:].rearrange("p q j -> p (q j)"), ALU.mult)
         minus_at = turn(0, "back", ("waht",))
         on_vector(scratch(0, "result"), made[0, "gated"], minus_at, ALU.subtract)
-        quantise(second[2:], "codes_third", round_pieces(second[2:], AT_STAGE_ZT + HALF))
+        quantise(second[:2], "codes_second", second_stage)
+        quantise(second[2:], "codes_third", third_stage)
         difference_on_gpsimd(2, bank="z")
+        late = (((2, WV),), ((2, WT), (3, WT), (2, ZV)), ((2, ZT), (3, WV), (3, ZV), (3, ZT)))
+        scalar_stage = round_pieces(late[2], "late_stage", (1,))
         by_entries(1, "hv", 0, WV, 1.0, bank="total0")
-        by_entries(1, "ht", 1, WT, -1.0, bank="z")
+        by_entries(1, "ht", 1, WT, -1.0)
+        gate(1)
         gated_on_gpsimd(2, "total0")
-        gate(1, "ht")
         place(0)
         gated_on_vector(1)
         mixed_on_vector(1)
-        by_gpsimd = ((2, WV), (3, WV), (2, WT))
-        by_scalar = ((2, ZT), (3, WT), (2, ZV), (3, ZV), (3, ZT))
-        gpsimd_stage = round_pieces(by_gpsimd, AT_STAGE_ZT + HALF)
-        scalar_stage = round_pieces(by_scalar, "late_stage", (1, 2, 3, 0, 4))
+        stages = [round_pieces(late[0], f"raw{WT}_1"), round_pieces(late[1], AT_RAW_ZT + HALF), scalar_stage]
+        round_into(scalar_stage, late[2], (2, 0, 3))
         weighed_on_vector(1, f"raw{ZT}_2")
-        quantise(by_gpsimd, "codes_late", gpsimd_stage)
-        quantise(by_scalar[:1], None, scalar_stage[:, :1, :])
-        quantise(by_scalar[1:], None, scalar_stage[:, 1:, :])
+        quantise(late[0], AT_MIXED, stages[0])
+        quantise(late[1], AT_MIXED + HALF, stages[1])
+        quantise(late[2], None, stages[2])
         place(1)
         last = len(STEPS) - 1
         for step in range(3, last + 1):
             difference_on_gpsimd(step, "late_stage" if step == 3 else None)
-            gated_on_gpsimd(step)
+            gated_on_gpsimd(step, "total0" if step >= 4 else None)
             if step == last:
                 nc.gpsimd.tensor_tensor(
                     scratch(step, "result")[:], made[step, "gated"][:], made[step, "aht"][:], ALU.add

from contextlib import ExitStack

import concourse.mybir as mybir
from concourse.masks import make_identity

K, N, T, J = 512, 512, 2048, 1024
FLOPS = 4 * 2 * K * N * J

F32 = mybir.dt.float32
BF16 = mybir.dt.bfloat16
I32 = mybir.dt.int32
U32 = mybir.dt.uint32
U16 = mybir.dt.uint16
U8 = mybir.dt.uint8
FP8X4 = mybir.dt.float8_e4m3fn_x4
ALU = mybir.AluOpType
ACT = mybir.ActivationFunctionType

P = 128
PACK = 4
HALF = 512
N_TILES = N // P
QUARTERS = HALF // P
LIST_COLS = HALF // 16
WV, WT, ZV, ZT = range(4)
BLOCKS = ((0, 1), (1, 2), (2, 4))
W_ROW = 8
PLANE_ROW = (0, 4)
FIRST_ZEROED = 1280
AT_RAW_ZT = 0
AT_STAGE_ZT = 6144
AT_MIXED = 10240
PAGE_OF = (0, 1, 2, 0)
STEPS = ((0, 0), (1, 0), (0, 1), (1, 1), (2, 0), (3, 0), (2, 1), (3, 1))
ROUNDERS = ("ssss", "vvss", "gggs", "sgss")


def tile_list_gmu_tanh_scat_kernel(
    tc, tab_words, tab_scales, tab2_words, tab2_scales, zv, zt, b, wv, wt, wgo, offs, offs2, out
):
    nc = tc.nc
    weights = (wv, wt, zv, zt)
    with ExitStack() as ctx:
        held = ctx.enter_context(tc.tile_pool(name="held", bufs=1))
        work = ctx.enter_context(tc.tile_pool(name="work", bufs=3))
        psum = ctx.enter_context(tc.psum_pool(name="psum", bufs=1))
        turns = ctx.enter_context(tc.tile_pool(name="turns", bufs=1))

        lists = [held.tile([P, J // 16], U16, name=f"list{a}") for a in range(2)]
        words = [held.tile([P, T], I32, name=f"words{a}", align_bytes=64) for a in range(2)]
        planes = [held.tile([P, T], U8, name=f"plane{a}") for a in range(2)]
        small = held.tile([P, P], F32, tag="small")
        ident = held.tile([P, P], F32)
        pages = [held.tile([P, T], F32, name=f"page{g}") for g in range(2)]
        for zeroed in (planes[0], ident, planes[1], small, *pages):
            nc.vector.memset(zeroed[:].bitcast(I32), 0)
        make_identity(nc, ident[:], nomemset=True)

        def placed(shape, dtype, name, where):
            if isinstance(where, int):
                return turns.tile(shape, dtype, name=name, offset=where, align_bytes=64)
            return held.tile(shape, dtype, name=name, tag=where or name, align_bytes=64)

        def load_table(a, table_words, table_scales):
            rows = table_scales[0].rearrange("(q r) t -> r q t", r=4)
            for r in range(4):
                nc.sync.dma_start(planes[a][PLANE_ROW[a] + r : P : 32, :].bitcast(I32), rows[r].bitcast(I32))
            nc.sync.dma_start(words[a][:], table_words[0].rearrange("p t i -> p (t i)").bitcast(I32))

        nc.sync.dma_start(lists[0][:], offs)
        nc.sync.dma_start(lists[1][:], offs2)
        load_table(0, tab_words, tab_scales)
        load_table(1, tab2_words, tab2_scales)
        nc.sync.dma_start(small[0:N_TILES, :], b.rearrange("(t p) -> t p", p=P))
        nc.sync.dma_start(small[W_ROW : W_ROW + J // P, :], wgo[0].rearrange("(t p) -> t p", p=P))
        raw = {}
        for t0, t1 in BLOCKS:
            for w in range(4):
                width = 1 if w == ZT else t1 - t0
                for first in range(t0, t1, width):
                    where = AT_RAW_ZT if (first, w) == (0, ZT) else None
                    block = placed([P, PACK, width * P], F32, f"raw{w}_{first}", where)
                    nc.sync.dma_start(
                        block[:], weights[w].rearrange("(p i) n -> p i n", i=PACK)[:, :, first * P : (first + width) * P]
                    )
                    for t in range(first, first + width):
                        raw[t, w] = block[:, :, (t - first) * P : (t - first + 1) * P]


        warm = held.tile([P, 1], F32)
        nc.scalar.activation(warm[:], ident[:, 0:1], ACT.Sigmoid)

        picked = {}
        picked_scales = {}

        def gather_words(a, h, tag):
            tile = placed([P, HALF], U32, f"gw{a}{h}", tag)
            entries = lists[a][:, h * LIST_COLS : (h + 1) * LIST_COLS]
            nc.vector.tensor_copy(tile[:], words[a][:].bitcast(U32).indirect(entries))
            picked[a, h] = tile

        def gather_scales(a, h, tag):
            tile = placed([P, HALF], U8, f"gs{a}{h}", tag)
            entries = lists[a][:, h * LIST_COLS : (h + 1) * LIST_COLS]
            nc.vector.tensor_copy(tile[:], planes[a][:].indirect(entries))
            picked_scales[a, h] = tile[PLANE_ROW[a] : P, :]

        codes = {}
        scales = {}

        def round_pieces(pieces, tag, chosen=None):
            t0, w0 = pieces[0]
            stage = placed([P, len(pieces), P * PACK], BF16, f"st{t0}{w0}", tag)
            round_into(stage, pieces, chosen or range(len(pieces)))
            return stage[:]

        def round_into(stage, pieces, chosen):
            for n in chosen:
                t, w = pieces[n]
                if ROUNDERS[t][w] == "g":
                    nc.gpsimd.tensor_scalar(
                        stage[:, n, :].rearrange("p (n i) -> p n i", i=PACK),
                        raw[t, w].rearrange("p i n -> p n i"),
                        1.0,
                        0.0,
                        ALU.mult,
                        ALU.add,
                    )
                else:
                    copy = nc.scalar.copy if ROUNDERS[t][w] == "s" else nc.vector.tensor_copy
                    copy(
                        stage[:, n, :].rearrange("p (c x i) -> p c i x", x=4, i=PACK),
                        raw[t, w].rearrange("p i (c x) -> p c i x", x=4),
                    )

        def quantise(pieces, codes_tag, stage):
            t0, w0 = pieces[0]
            group_codes = placed([P, len(pieces), P], U32, f"q{t0}{w0}", codes_tag)
            group_scales = held.tile([P, len(pieces), P], U8, name=f"qs{t0}{w0}", align_bytes=64)
            nc.vector.quantize_mx(
                out=group_codes[:].rearrange("p w n -> p (w n)").bitcast(FP8X4),
                scales=group_scales[:].rearrange("p w n -> p (w n)"),
                in_=stage.rearrange("p w n -> p (w n)"),
            )
            for n, piece in enumerate(pieces):
                codes[piece] = group_codes[:, n, :]
                scales[piece] = group_scales[:, n, :]

        made = {}

        def scratch(step, name, tag=None):
            if tag is None:
                made[step, name] = work.tile([P, HALF], F32, name=f"{name}{step}", tag=name)
            else:
                made[step, name] = placed([P, HALF], F32, f"{name}{step}", tag)
            return made[step, name]

        def by_features(step, name, passes, tag=None, bank=None):
            t, h = STEPS[step]
            acc = psum.tile([P, HALF], F32, name=f"{name}{step}", tag=bank or name)
            for n, (a, w) in enumerate(passes):
                nc.tensor.matmul_mx(
                    out=acc[:],
                    lhsT=codes[t, w].bitcast(FP8X4),
                    lhsT_scale=scales[t, w],
                    rhs=picked[a, h][:].bitcast(FP8X4),
                    rhs_scale=picked_scales[a, h],
                    start=(n == 0),
                    stop=(n == len(passes) - 1),
                )
            if name == "z":
                nc.scalar.activation(scratch(step, "gate", tag)[:], acc[:], ACT.Sigmoid, bias=bias[:, t : t + 1])
            else:
                nc.scalar.activation(scratch(step, f"a{name}", tag)[:], acc[:], ACT.Tanh)

        def by_entries(step, name, a, w, sign, tag=None, bank=None):
            t, h = STEPS[step]
            acc = psum.tile([P, QUARTERS, P], F32, name=f"{name}{step}", tag=bank or name)
            for q in range(QUARTERS):
                nc.tensor.matmul_mx(
                    out=acc[:, q, :],
                    lhsT=picked[a, h][:, q * P : (q + 1) * P].bitcast(FP8X4),
                    lhsT_scale=picked_scales[a, h][:, q * P : (q + 1) * P],
                    rhs=codes[t, w].bitcast(FP8X4),
                    rhs_scale=scales[t, w],
                    start=True,
                    stop=True,
                )
            act = scratch(step, f"a{name}", tag)
            flat = acc[:].rearrange("p q j -> p (q j)")
            parts = 2 if step == 0 else 1
            for part in range(parts):
                cols = slice(part * HALF // parts, (part + 1) * HALF // parts)
                nc.scalar.activation(act[:, cols], flat[:, cols], ACT.Tanh, scale=sign)

        def weigh_entries(step, name, tag=None):
            h = STEPS[step][1]
            weighed = scratch(step, f"w{name}", tag)
            for q in range(QUARTERS):
                col = h * QUARTERS + q
                cols = slice(q * P, (q + 1) * P)
                nc.scalar.activation(
                    weighed[:, cols], made[step, name][:, cols], ACT.Copy, scale=w_cols[:, col : col + 1]
                )

        def add_turned(acc, source, first, last):
            for q in range(QUARTERS):
                nc.tensor.matmul(
                    acc[:, q, :],
                    source[:, q * P : (q + 1) * P],
                    ident[:],
                    start=(first and q == 0),
                    stop=(last and q == QUARTERS - 1),
                    is_transpose=True,
                )

        def on_vector(target, left, right, op):
            for cols in (slice(0, HALF // 2), slice(HALF // 2, HALF)):
                nc.vector.tensor_tensor(target[:, cols], left[:, cols], right[:, cols], op)

        def gate(step, bank=None, tag=None):
            by_features(step, "z", ((0, ZV), (1, ZT)), tag, bank)

        def turn(step, bank, names):
            turn_of_bank = 1 if bank == "total" and step >= 3 else step % 2
            acc = psum.tile([P, QUARTERS, P], F32, name=f"{bank}{step}", tag=f"{bank}{turn_of_bank}")
            for q in range(QUARTERS):
                for n, name in enumerate(names):
                    nc.tensor.matmul(
                        acc[:, q, :],
                        made[step, name][:, q * P : (q + 1) * P],
                        ident[:],
                        start=(n == 0),
                        stop=(n == len(names) - 1),
                        is_transpose=True,
                    )
            return acc[:].rearrange("p q j -> p (q j)")

        def gated_on_vector(step):
            difference = turn(step, "total", ("aht", "ahv"))
            on_vector(scratch(step, "gated"), made[step, "gate"], difference, ALU.mult)

        def mixed_on_vector(step):
            minus_at = turn(step, "back", ("aht",))
            on_vector(scratch(step, "diff", AT_MIXED), made[step, "gated"], minus_at, ALU.subtract)

        def weighed_on_vector(step, tag=None):
            h = STEPS[step][1]
            spread = psum.tile([P, QUARTERS, P], F32, name=f"spread{step}", tag="turned")
            for q in range(QUARTERS):
                col = h * QUARTERS + q
                nc.tensor.transpose(spread[:, q, :], w_cols[:, col : col + 1].to_broadcast([P, P]), ident[:])
            on_vector(scratch(step, "result", tag), made[step, "diff"], spread[:].rearrange("p q j -> p (q j)"), ALU.mult)

        def difference_on_gpsimd(step, tag=None, bank=None):
            by_features(step, "hv", ((0, WV),))
            by_features(step, "ht", ((1, WT),), bank=bank)
            diff = scratch(step, "diff", tag)
            nc.gpsimd.tensor_tensor(diff[:], made[step, "ahv"][:], made[step, "aht"][:], ALU.subtract)

        def gated_on_gpsimd(step, bank=None):
            gate(step, bank)
            nc.gpsimd.tensor_tensor(scratch(step, "gated")[:], made[step, "diff"][:], made[step, "gate"][:], ALU.mult)

        def weighed_by_entries(step):
            h = STEPS[step][1]
            total = turn(step, "total", ("gated", "aht"))
            weighed = scratch(step, "weighed", "w_rows" if step == len(STEPS) - 2 else None)
            for q in range(QUARTERS):
                col = h * QUARTERS + q
                cols = slice(q * P, (q + 1) * P)
                nc.scalar.activation(weighed[:, cols], total[:, cols], ACT.Copy, scale=w_cols[:, col : col + 1])
            nc.scalar.copy(scratch(step, "result")[:], turn(step, "back", ("weighed",)))

        def place(step):
            t, h = STEPS[step]
            page = pages[PAGE_OF[t]]
            places = page[:].indirect(lists[0][:, h * LIST_COLS : (h + 1) * LIST_COLS])
            if step == len(STEPS) - 1:
                nc.vector.tensor_tensor(places, made[step, "result"][:], w_rows[:], ALU.mult)
            else:
                nc.vector.tensor_copy(places, made[step, "result"][:])
            if h == 1:
                nc.sync.dma_start(out[t * P : (t + 1) * P, :], page[:])

        gather_scales(0, 0, "gs00")
        gather_scales(0, 1, "gs01")
        gather_words(0, 0, "gw00")
        gather_scales(1, 0, "gs10")
        gather_words(1, 0, "gw10")
        turned = psum.tile([P, P], F32, tag="turned")
        nc.tensor.transpose(turned[:], small[:], ident[:])
        columns = held.tile([P, W_ROW + J // P], F32)
        nc.scalar.copy(columns[:], turned[:, 0 : W_ROW + J // P])
        pages.append(held.tile([P, T], F32, name="page2", tag="small"))
        bias = columns[:, 0:N_TILES]
        w_cols = columns[:, W_ROW:]
        for w in range(4):
            quantise(((0, w),), f"codes{w}", round_pieces(((0, w),), AT_STAGE_ZT if w == ZT else f"stage{w}"))
        for cols in (slice(0, FIRST_ZEROED), slice(FIRST_ZEROED, T)):
            nc.vector.memset(pages[2][:, cols].bitcast(I32), 0)
        gather_words(0, 1, f"raw{WT}_0")
        gather_scales(1, 1, AT_RAW_ZT)
        gather_words(1, 1, AT_STAGE_ZT - 3 * HALF)
        second = tuple((1, w) for w in range(4))
        second_stage = round_pieces(second[:2], AT_STAGE_ZT + HALF)

        by_entries(0, "hv", 0, WV, 1.0, AT_RAW_ZT + HALF)
        weigh_entries(0, "ahv")
        by_entries(0, "ht", 1, WT, -1.0)
        weigh_entries(0, "aht", "late_stage")
        gate(0, tag="codes_second")
        third_stage = round_pieces(second[2:], AT_RAW_ZT + HALF)
        first_difference = psum.tile([P, QUARTERS, P], F32, tag="total0")
        add_turned(first_difference, made[0, "wahv"], True, False)
        add_turned(first_difference, made[0, "waht"], False, True)
        on_vector(scratch(0, "gated", "codes_third"), made[0, "gate"], first_difference[:].rearrange("p q j -> p (q j)"), ALU.mult)
        minus_at = turn(0, "back", ("waht",))
        on_vector(scratch(0, "result"), made[0, "gated"], minus_at, ALU.subtract)
        quantise(second[:2], "codes_second", second_stage)
        quantise(second[2:], "codes_third", third_stage)
        difference_on_gpsimd(2, bank="z")
        late = (((2, WV),), ((2, WT), (3, WT), (2, ZV)), ((2, ZT), (3, WV), (3, ZV), (3, ZT)))
        scalar_stage = round_pieces(late[2], "late_stage", (1,))
        by_entries(1, "hv", 0, WV, 1.0, bank="total0")
        by_entries(1, "ht", 1, WT, -1.0)
        gate(1)
        gated_on_gpsimd(2, "total0")
        place(0)
        gated_on_vector(1)
        mixed_on_vector(1)
        stages = [round_pieces(late[0], f"raw{WT}_1"), round_pieces(late[1], AT_RAW_ZT + HALF), scalar_stage]
        round_into(scalar_stage, late[2], (2, 0, 3))
        weighed_on_vector(1, f"raw{ZT}_2")
        quantise(late[0], AT_MIXED, stages[0])
        quantise(late[1], AT_MIXED + HALF, stages[1])
        quantise(late[2], None, stages[2])
        place(1)
        last = len(STEPS) - 1
        for step in range(3, last + 1):
            difference_on_gpsimd(step, "late_stage" if step == 3 else None)
            gated_on_gpsimd(step, "total0" if step >= 4 else None)
            if step == last:
                nc.gpsimd.tensor_tensor(
                    scratch(step, "result")[:], made[step, "gated"][:], made[step, "aht"][:], ALU.add
                )
            weighed_by_entries(step - 1)
            if step == last:
                w_rows = held.tile([P, HALF], F32, tag="w_rows", align_bytes=64)
                nc.sync.dma_start(w_rows[:], wgo[:, STEPS[last][1] * HALF : (STEPS[last][1] + 1) * HALF])
            place(step - 1)
        place(last)
